import numpy as np
import ml_dtypes


def mxq(x, axis, fmt="e4m3"):
    dtype, down = {"e4m3": (ml_dtypes.float8_e4m3fn, 7), "e5m2": (ml_dtypes.float8_e5m2, 14)}[fmt]
    v = np.moveaxis(np.asarray(x, np.float32).astype(ml_dtypes.bfloat16).astype(np.float64), axis, -1)
    blocks = v.reshape(v.shape[:-1] + (-1, 32))
    amax = np.abs(blocks).max(-1, keepdims=True)
    byte = np.maximum(np.where(amax > 0, np.frexp(amax)[1] - 1 + 127, 0) - down, 1)
    scale = np.exp2(byte - 127.0)
    codes = (blocks / scale).astype(np.float32).astype(dtype).astype(np.float64)
    return np.moveaxis((codes * scale).reshape(v.shape), -1, axis)


WIDE = False


def mx_kscale(k):
    if not WIDE:
        return np.ones(k)
    levels = np.array([10, -10, 5, -5, 0])
    if k % 512:
        return np.exp2(np.random.permutation(np.resize(levels, k // 32))).repeat(32)
    a = np.empty((k // 512, 16))
    for p in range(k // 512):
        a[p, :8] = np.random.permutation(np.resize(levels, 8))
        for g in range(8):
            far = levels[np.abs(levels - a[p, g]) >= 10]
            a[p, g + 8] = far[np.random.randint(len(far))]
    return np.exp2(a.ravel()).repeat(32)


def f64(x):
    return np.asarray(x).astype(np.float64)


def striped(idx):
    return np.tile(idx.reshape(-1, 16).T, (8, 1)).astype(np.uint16)


def unstriped(offs):
    return offs[:16].T.reshape(-1).astype(np.int64)


E2M1 = np.array([0.0, 0.5, 1.0, 1.5, 2.0, 3.0, 4.0, 6.0, -0.0, -0.5, -1.0, -1.5, -2.0, -3.0, -4.0, -6.0])


def pack_weight(w, fmt):
    k, n = w.shape
    w = f64(np.asarray(w, np.float32).astype(ml_dtypes.bfloat16)).reshape(k // 32, 32, n)
    amax = np.abs(w).max(1)
    if fmt == "e4m3":
        byte = np.frexp(amax)[1] - 1 + 127 - 7
    else:
        mant, ex = np.frexp(amax / 6.0)
        byte = np.where(mant > 0.5, ex, ex - 1) + 127
    byte = np.clip(np.where(amax > 0, byte, 1), 1, 254)
    scaled = (w * np.exp2(127.0 - byte)[:, None, :]).reshape(k, n).astype(np.float32)
    by_word = np.ascontiguousarray(scaled.reshape(k // 512, 128, 4, n).transpose(0, 1, 3, 2))
    if fmt == "e4m3":
        words = by_word.astype(ml_dtypes.float8_e4m3fn).view(np.uint8)
    else:
        c = by_word.astype(ml_dtypes.float4_e2m1fn).view(np.uint8) & 0xF
        words = (c[..., 0::2] | (c[..., 1::2] << 4)).reshape(k // 512, 128, 2 * n)
    return np.ascontiguousarray(words), np.ascontiguousarray(byte.astype(np.uint8).reshape(k // 512, 16, n))


def unpack_weight(words, scales, fmt):
    g, _, n = scales.shape
    words = np.ascontiguousarray(words).reshape(g, 128, n, -1)
    if fmt == "e4m3":
        vals = words.view(ml_dtypes.float8_e4m3fn).astype(np.float64)
    else:
        nib = np.empty((g, 128, n, 4), np.uint8)
        nib[..., 0::2] = words & 0xF
        nib[..., 1::2] = words >> 4
        vals = E2M1[nib]
    vals = vals * np.repeat(np.exp2(scales.astype(np.float64) - 127.0), 8, axis=1)[..., None]
    return vals.transpose(0, 1, 3, 2).reshape(g * 512, n)


def silu(v):
    return v / (1.0 + np.exp(-np.maximum(v, -700.0)))


K, M, T, S = 1024, 512, 4096, 1536


def setup_inputs():
    n = np.random.standard_normal
    s = mx_kscale(K)[:, None]
    u = mx_kscale(512)[:, None]
    v = pack_weight(n((K, T)) * s, "e4m3")
    p_w2 = pack_weight(1.4 * n((512, M)) / np.sqrt(512) / u, "e2m1")
    return {
        "tab_words": v[0],
        "tab_scales": v[1],
        "w1": (n((K, 512)) / np.sqrt(K) / s * u.T).astype(np.float32),
        "w2_words": p_w2[0],
        "w2_scales": p_w2[1],
        "rT": n((M, T)).astype(np.float32),
        "b": (0.3 * n(512)).astype(np.float32),
        "offs": striped(np.random.permutation(T)[:S]),
    }


def reference(tab_words, tab_scales, w1, w2_words, w2_scales, rT, b, offs):
    tab_ = unpack_weight(tab_words, tab_scales, "e4m3")[:, unstriped(offs)]
    w1_ = mxq(f64(w1), 0, "e4m3")
    w2_ = unpack_weight(w2_words, w2_scales, "e2m1")
    h_ = mxq(np.maximum(w1_.T @ tab_, 0.0), 0, "e4m3")
    y = w2_.T @ h_
    return (silu(y + f64(b)[:, None])) + f64(rT)[:, unstriped(offs)]

@@ -1,0 +1,159 @@
+from contextlib import ExitStack
+
+import concourse.mybir as mybir
+from concourse.masks import make_identity
+
+K, M, T, S, H = 1024, 512, 4096, 1536, 512
+FLOPS = 2 * S * (K * H + H * M)
+
+F32 = mybir.dt.float32
+BF16 = mybir.dt.bfloat16
+I32 = mybir.dt.int32
+U32 = mybir.dt.uint32
+U16 = mybir.dt.uint16
+U8 = mybir.dt.uint8
+FP8X4 = mybir.dt.float8_e4m3fn_x4
+FP4X4 = mybir.dt.float4_e2m1fn_x4
+ACT = mybir.ActivationFunctionType
+ADD = mybir.AluOpType.add
+
+P = 128
+PACK = 4
+PASSES = K // (P * PACK)
+CHUNK = 512
+CHUNKS = S // CHUNK
+GROUP = CHUNK // PACK
+ROW_TILES = M // P
+QUADS = 4
+
+
+def tile_list_tabres_silu_kernel(tc, tab_words, tab_scales, w1, w2_words, w2_scales, rT, b, offs, out):
+    nc = tc.nc
+    with ExitStack() as ctx:
+        keep = ctx.enter_context(tc.tile_pool(name="keep", bufs=1))
+        h_banks = ctx.enter_context(tc.psum_pool(name="h_banks", bufs=6))
+        y_banks = ctx.enter_context(tc.psum_pool(name="y_banks", bufs=1))
+
+        offsets = keep.tile([P, S // 16], U16, name="offsets")
+        nc.sync.dma_start(offsets[:], offs)
+
+        def picks(c):
+            return offsets[:, c * CHUNK // 16 : (c + 1) * CHUNK // 16]
+
+        tab_plane = keep.tile([P, T], U8, name="tab_plane", align_bytes=64)
+        nc.vector.memset(tab_plane[:].bitcast(I32), 0)
+
+        tab = [keep.tile([P, T], I32, name=f"tab{a}", align_bytes=64) for a in range(PASSES)]
+        w1_raw = [keep.tile([P, PACK, H], F32, name=f"w1_raw{a}") for a in range(PASSES)]
+        resid = [keep.tile([P, T], F32, name=f"resid{m}", align_bytes=64) for m in range(ROW_TILES)]
+        w2_codes = keep.tile([P, 2 * M], U8, name="w2_codes", align_bytes=64)
+        w2_plane = keep.tile([P, M], U8, name="w2_plane", align_bytes=64)
+
+        def load_tab(a):
+            nc.sync.dma_start(out=tab[a][:], in_=tab_words[a].rearrange("p t i -> p (t i)").bitcast(I32))
+
+        bias_rows = keep.tile([P, P], F32, name="bias_rows")
+        identity = keep.tile([P, P], F32, name="identity")
+        bias = keep.tile([P, ROW_TILES], F32, name="bias")
+        nc.gpsimd.memset(w2_plane[:].bitcast(I32), 0)
+        nc.gpsimd.memset(bias_rows[:], 0.0)
+        make_identity(nc, identity[:])
+
+        load_tab(0)
+        nc.sync.dma_start(out=bias_rows[0:ROW_TILES, :], in_=b.rearrange("(m p) -> m p", p=P))
+        for a in range(PASSES):
+            for q in range(QUADS):
+                nc.sync.dma_start(
+                    out=tab_plane[32 * q + 4 * a : 32 * q + 4 * a + 4, :].bitcast(I32),
+                    in_=tab_scales[a, 4 * q : 4 * q + 4, :].bitcast(I32),
+                )
+            nc.sync.dma_start(out=w1_raw[a][:], in_=w1[512 * a : 512 * (a + 1), :].rearrange("(p j) c -> p j c", j=PACK))
+        load_tab(1)
+        nc.sync.dma_start(out=w2_codes[:].bitcast(I32), in_=w2_words[0].bitcast(I32))
+        for q in range(QUADS):
+            nc.sync.dma_start(
+                out=w2_plane[32 * q : 32 * q + 4, :].bitcast(I32),
+                in_=w2_scales[0, 4 * q : 4 * q + 4, :].bitcast(I32),
+            )
+        for m in range(ROW_TILES):
+            nc.sync.dma_start(out=resid[m][:], in_=rT[P * m : P * (m + 1), :])
+
+        v_plane = [keep.tile([P, CHUNK], U8, name=f"v_plane{c}", align_bytes=64) for c in range(CHUNKS)]
+        v_codes = [[keep.tile([P, CHUNK], U32, name=f"v_codes{a}_{c}", align_bytes=64) for c in range(CHUNKS)] for a in range(PASSES)]
+        w1_bf = [keep.tile([P, PACK * H], BF16, name=f"w1_bf{a}", align_bytes=64) for a in range(PASSES)]
+        w1_codes = [keep.tile([P, H], U32, name=f"w1_codes{a}", align_bytes=64) for a in range(PASSES)]
+        w1_plane = [keep.tile([P, H], U8, name=f"w1_plane{a}", align_bytes=64) for a in range(PASSES)]
+        h_bf = [keep.tile([P, PACK * CHUNK], BF16, name=f"h_bf{c}", align_bytes=64) for c in range(CHUNKS)]
+        h_codes = [keep.tile([P, CHUNK], U32, name=f"h_codes{c}", align_bytes=64) for c in range(CHUNKS)]
+        h_plane = [keep.tile([P, CHUNK], U8, name=f"h_plane{c}", align_bytes=64) for c in range(CHUNKS)]
+        result = [keep.tile([P, S], F32, name=f"result{m}") for m in range(ROW_TILES)]
+
+        def gather_words(a, c):
+            nc.vector.tensor_copy(out=v_codes[a][c][:], in_=tab[a][:].bitcast(U32).indirect(picks(c)))
+
+        bias_bank = y_banks.tile([P, P], F32, name="bias_bank", tag="y1")
+        nc.tensor.transpose(bias_bank[:], bias_rows[:], identity[:])
+        nc.scalar.copy(out=bias[:], in_=bias_bank[:, 0:ROW_TILES])
+        for c in range(CHUNKS):
+            gather_words(0, c)
+        for c in range(CHUNKS):
+            nc.vector.tensor_copy(out=v_plane[c][:], in_=tab_plane[:].indirect(picks(c)))
+        for a in range(PASSES):
+            nc.scalar.copy(
+                out=w1_bf[a][:].rearrange("p (t m j) -> p m t j", t=PACK, j=PACK),
+                in_=w1_raw[a][:].rearrange("p j (m t) -> p m t j", t=PACK),
+            )
+            nc.vector.quantize_mx(out=w1_codes[a][:].bitcast(FP8X4), scales=w1_plane[a][:], in_=w1_bf[a][:])
+
+        def first_layer(c):
+            for g in range(CHUNK // GROUP):
+                cols = slice(g * GROUP, (g + 1) * GROUP)
+                bank = h_banks.tile([P, PACK, GROUP], F32, name="h_bank")
+                for a in range(PASSES):
+                    for t in range(PACK):
+                        nc.tensor.matmul_mx(
+                            out=bank[:, t, :],
+                            lhsT=w1_codes[a][:, P * t : P * (t + 1)].bitcast(FP8X4),
+                            lhsT_scale=w1_plane[a][:, P * t : P * (t + 1)],
+                            rhs=v_codes[a][c][:, cols].bitcast(FP8X4),
+                            rhs_scale=v_plane[c][4 * a : P, cols],
+                            start=(a == 0 and t == 0),
+                            stop=(a == PASSES - 1 and t == PACK - 1),
+                        )
+                woven = h_bf[c][:, PACK * GROUP * g : PACK * GROUP * (g + 1)].rearrange("p (n t) -> p n t", t=PACK)
+                sums = bank[:].rearrange("p t n -> p n t")
+                if c == 1 and g % 2 == 0:
+                    nc.vector.tensor_scalar_max(woven, sums, 0.0)
+                else:
+                    nc.scalar.activation(out=woven, in_=sums, func=ACT.Relu)
+            nc.vector.quantize_mx(out=h_codes[c][:].bitcast(FP8X4), scales=h_plane[c][:], in_=h_bf[c][:])
+
+        def second_layer(m, c):
+            step = m * CHUNKS + c
+            bank = y_banks.tile([P, CHUNK], F32, name="y_bank", tag=f"y{step % 2}")
+            nc.tensor.matmul_mx(
+                out=bank[:],
+                lhsT=w2_codes[:, 2 * P * m : 2 * P * (m + 1)].bitcast(FP4X4),
+                lhsT_scale=w2_plane[:, P * m : P * (m + 1)],
+                rhs=h_codes[c][:].bitcast(FP8X4),
+                rhs_scale=h_plane[c][:],
+                start=True,
+                stop=True,
+            )
+            act = keep.tile([P, CHUNK], F32, name="act", tag=f"act{step % 2}")
+            nc.scalar.activation(out=act[:], in_=bank[:], func=ACT.Silu, bias=bias[:, m : m + 1])
+            cols = slice(c * CHUNK, (c + 1) * CHUNK)
+            nc.vector.tensor_tensor(out=result[m][:, cols], in0=resid[m][:].indirect(picks(c)), in1=act[:], op=ADD)
+            if m == ROW_TILES - 1:
+                nc.sync.dma_start(out=out[P * m : P * (m + 1), cols], in_=result[m][:, cols])
+            elif c == CHUNKS - 1:
+                nc.sync.dma_start(out=out[P * m : P * (m + 1), :], in_=result[m][:])
+
+        for c in range(CHUNKS):
+            gather_words(1, c)
+        for c in range(CHUNKS):
+            first_layer(c)
+            second_layer(0, c)
+        for m in range(1, ROW_TILES):
+            for c in range(CHUNKS):
+                second_layer(m, c)

@@ -31,44 +31,78 @@ def tile_list_tabres_silu_kernel(tc, tab_words, tab_scales, w1, w2_words, w2_sca
     nc = tc.nc
     with ExitStack() as ctx:
         keep = ctx.enter_context(tc.tile_pool(name="keep", bufs=1))
-        h_banks = ctx.enter_context(tc.psum_pool(name="h_banks", bufs=6))
-        y_banks = ctx.enter_context(tc.psum_pool(name="y_banks", bufs=1))
+        banks = ctx.enter_context(tc.psum_pool(name="banks", bufs=1))
 
         offsets = keep.tile([P, S // 16], U16, name="offsets")
-        nc.sync.dma_start(offsets[:], offs)
 
         def picks(c):
             return offsets[:, c * CHUNK // 16 : (c + 1) * CHUNK // 16]
 
-        tab_plane = keep.tile([P, T], U8, name="tab_plane", align_bytes=64)
-        nc.vector.memset(tab_plane[:].bitcast(I32), 0)
-
-        tab = [keep.tile([P, T], I32, name=f"tab{a}", align_bytes=64) for a in range(PASSES)]
+        tab_rows = keep.tile([P, T], U8, name="tab_rows", align_bytes=64)
+        v_rows = keep.tile([P, S], U8, name="v_rows", align_bytes=64)
+        v_plane = [keep.tile([P, S], U8, name=f"v_plane{a}", align_bytes=64) for a in range(PASSES)]
+        tab = [keep.tile([P, T], I32, name=f"tab{a}", tag=f"tab{a}", align_bytes=64) for a in range(PASSES)]
         w1_raw = [keep.tile([P, PACK, H], F32, name=f"w1_raw{a}") for a in range(PASSES)]
         resid = [keep.tile([P, T], F32, name=f"resid{m}", align_bytes=64) for m in range(ROW_TILES)]
         w2_codes = keep.tile([P, 2 * M], U8, name="w2_codes", align_bytes=64)
         w2_plane = keep.tile([P, M], U8, name="w2_plane", align_bytes=64)
+        bias_rows = keep.tile([P, P], F32, name="bias_rows")
+        identity = keep.tile([P, P], F32, name="identity")
+        bias = keep.tile([P, ROW_TILES], F32, name="bias")
+        w1_bf = [keep.tile([P, PACK * H], BF16, name=f"w1_bf{a}", tag=f"w1_bf{a}", align_bytes=64) for a in range(PASSES)]
+        v_codes = [[None] * CHUNKS for a in range(PASSES)]
+        w1_codes = [keep.tile([P, H], U32, name=f"w1_codes{a}", align_bytes=64) for a in range(PASSES)]
+        w1_plane = [None] * PASSES
+        h_bf = [keep.tile([P, PACK * CHUNK], BF16, name=f"h_bf{c}", align_bytes=64) for c in range(CHUNKS)]
+        h_codes = [keep.tile([P, CHUNK], U32, name=f"h_codes{c}", align_bytes=64) for c in range(CHUNKS)]
+        h_plane = [keep.tile([P, CHUNK], U8, name=f"h_plane{c}", align_bytes=64) for c in range(CHUNKS)]
+        result = [keep.tile([P, S], F32, name=f"result{m}") for m in range(ROW_TILES)]
+
+        nc.vector.memset(tab_rows[:].bitcast(I32), 0)
+        nc.gpsimd.memset(bias_rows[:], 0.0)
+        for a in range(PASSES):
+            nc.gpsimd.memset(v_plane[a][:].bitcast(I32), 0)
+        nc.gpsimd.memset(w2_plane[:].bitcast(I32), 0)
+        make_identity(nc, identity[:])
 
         def load_tab(a):
             nc.sync.dma_start(out=tab[a][:], in_=tab_words[a].rearrange("p t i -> p (t i)").bitcast(I32))
 
-        bias_rows = keep.tile([P, P], F32, name="bias_rows")
-        identity = keep.tile([P, P], F32, name="identity")
-        bias = keep.tile([P, ROW_TILES], F32, name="bias")
-        nc.gpsimd.memset(w2_plane[:].bitcast(I32), 0)
-        nc.gpsimd.memset(bias_rows[:], 0.0)
-        make_identity(nc, identity[:])
-
-        load_tab(0)
-        nc.sync.dma_start(out=bias_rows[0:ROW_TILES, :], in_=b.rearrange("(m p) -> m p", p=P))
-        for a in range(PASSES):
-            for q in range(QUADS):
-                nc.sync.dma_start(
-                    out=tab_plane[32 * q + 4 * a : 32 * q + 4 * a + 4, :].bitcast(I32),
-                    in_=tab_scales[a, 4 * q : 4 * q + 4, :].bitcast(I32),
-                )
+        def load_w1(a):
             nc.sync.dma_start(out=w1_raw[a][:], in_=w1[512 * a : 512 * (a + 1), :].rearrange("(p j) c -> p j c", j=PACK))
+
+        def place_scale_rows(a):
+            for r in range(4):
+                nc.sync.dma_start(
+                    out=v_plane[a][4 * a + r : P : 32, :].bitcast(I32),
+                    in_=v_rows[64 * a + 4 * r : 64 * (a + 1) : 16, :].bitcast(I32),
+                )
+
+        def gather_words(a, c):
+            tag = "w1_bf1" if (a, c) == (1, 0) else f"v_codes{a}_{c}"
+            v_codes[a][c] = keep.tile([P, CHUNK], U32, name=f"v_codes{a}_{c}", tag=tag, align_bytes=64)
+            nc.vector.tensor_copy(out=v_codes[a][c][:], in_=tab[a][:].bitcast(U32).indirect(picks(c)))
+
+        def round_w1(a):
+            nc.scalar.copy(
+                out=w1_bf[a][:].rearrange("p (t m j) -> p m t j", t=PACK, j=PACK),
+                in_=w1_raw[a][:].rearrange("p j (m t) -> p m t j", t=PACK),
+            )
+
+        def quantise_w1(a):
+            w1_plane[a] = keep.tile([P, H], U8, name=f"w1_plane{a}", tag="tab0" if a == 0 else "w1_plane", align_bytes=64)
+            nc.vector.quantize_mx(out=w1_codes[a][:].bitcast(FP8X4), scales=w1_plane[a][:], in_=w1_bf[a][:])
+
+        load_w1(0)
+        nc.sync.dma_start(offsets[:], offs)
+        nc.sync.dma_start(out=tab_rows[0:P:4, :].bitcast(I32), in_=tab_scales.rearrange("a q t -> (a q) t").bitcast(I32))
+        load_tab(0)
+        load_w1(1)
+        nc.sync.dma_start(out=bias_rows[0:ROW_TILES, :], in_=b.rearrange("(m p) -> m p", p=P))
+        nc.vector.tensor_copy(out=v_rows[:], in_=tab_rows[:].indirect(offsets[:]))
+        place_scale_rows(0)
         load_tab(1)
+        place_scale_rows(1)
         nc.sync.dma_start(out=w2_codes[:].bitcast(I32), in_=w2_words[0].bitcast(I32))
         for q in range(QUADS):
             nc.sync.dma_start(
@@ -78,37 +112,21 @@ def tile_list_tabres_silu_kernel(tc, tab_words, tab_scales, w1, w2_words, w2_sca
         for m in range(ROW_TILES):
             nc.sync.dma_start(out=resid[m][:], in_=rT[P * m : P * (m + 1), :])
 
-        v_plane = [keep.tile([P, CHUNK], U8, name=f"v_plane{c}", align_bytes=64) for c in range(CHUNKS)]
-        v_codes = [[keep.tile([P, CHUNK], U32, name=f"v_codes{a}_{c}", align_bytes=64) for c in range(CHUNKS)] for a in range(PASSES)]
-        w1_bf = [keep.tile([P, PACK * H], BF16, name=f"w1_bf{a}", align_bytes=64) for a in range(PASSES)]
-        w1_codes = [keep.tile([P, H], U32, name=f"w1_codes{a}", align_bytes=64) for a in range(PASSES)]
-        w1_plane = [keep.tile([P, H], U8, name=f"w1_plane{a}", align_bytes=64) for a in range(PASSES)]
-        h_bf = [keep.tile([P, PACK * CHUNK], BF16, name=f"h_bf{c}", align_bytes=64) for c in range(CHUNKS)]
-        h_codes = [keep.tile([P, CHUNK], U32, name=f"h_codes{c}", align_bytes=64) for c in range(CHUNKS)]
-        h_plane = [keep.tile([P, CHUNK], U8, name=f"h_plane{c}", align_bytes=64) for c in range(CHUNKS)]
-        result = [keep.tile([P, S], F32, name=f"result{m}") for m in range(ROW_TILES)]
-
-        def gather_words(a, c):
-            nc.vector.tensor_copy(out=v_codes[a][c][:], in_=tab[a][:].bitcast(U32).indirect(picks(c)))
-
-        bias_bank = y_banks.tile([P, P], F32, name="bias_bank", tag="y1")
-        nc.tensor.transpose(bias_bank[:], bias_rows[:], identity[:])
-        nc.scalar.copy(out=bias[:], in_=bias_bank[:, 0:ROW_TILES])
+        round_w1(0)
         for c in range(CHUNKS):
             gather_words(0, c)
-        for c in range(CHUNKS):
-            nc.vector.tensor_copy(out=v_plane[c][:], in_=tab_plane[:].indirect(picks(c)))
-        for a in range(PASSES):
-            nc.scalar.copy(
-                out=w1_bf[a][:].rearrange("p (t m j) -> p m t j", t=PACK, j=PACK),
-                in_=w1_raw[a][:].rearrange("p j (m t) -> p m t j", t=PACK),
-            )
-            nc.vector.quantize_mx(out=w1_codes[a][:].bitcast(FP8X4), scales=w1_plane[a][:], in_=w1_bf[a][:])
+        quantise_w1(0)
+        round_w1(1)
+        bias_bank = banks.tile([P, P], F32, name="bias_bank", tag="bank7")
+        nc.tensor.transpose(bias_bank[:], bias_rows[:], identity[:])
+        nc.scalar.copy(out=bias[:], in_=bias_bank[:, 0:ROW_TILES])
+        quantise_w1(1)
 
         def first_layer(c):
             for g in range(CHUNK // GROUP):
                 cols = slice(g * GROUP, (g + 1) * GROUP)
-                bank = h_banks.tile([P, PACK, GROUP], F32, name="h_bank")
+                group = c * (CHUNK // GROUP) + g
+                bank = banks.tile([P, PACK, GROUP], F32, name="h_bank", tag=f"bank{group if group < 8 else group - 6}")
                 for a in range(PASSES):
                     for t in range(PACK):
                         nc.tensor.matmul_mx(
@@ -116,13 +134,13 @@ def tile_list_tabres_silu_kernel(tc, tab_words, tab_scales, w1, w2_words, w2_sca
                             lhsT=w1_codes[a][:, P * t : P * (t + 1)].bitcast(FP8X4),
                             lhsT_scale=w1_plane[a][:, P * t : P * (t + 1)],
                             rhs=v_codes[a][c][:, cols].bitcast(FP8X4),
-                            rhs_scale=v_plane[c][4 * a : P, cols],
+                            rhs_scale=v_plane[a][4 * a : P, c * CHUNK + g * GROUP : c * CHUNK + (g + 1) * GROUP],
                             start=(a == 0 and t == 0),
                             stop=(a == PASSES - 1 and t == PACK - 1),
                         )
                 woven = h_bf[c][:, PACK * GROUP * g : PACK * GROUP * (g + 1)].rearrange("p (n t) -> p n t", t=PACK)
                 sums = bank[:].rearrange("p t n -> p n t")
-                if c == 1 and g % 2 == 0:
+                if c > 0 and g % 2 == 0:
                     nc.vector.tensor_scalar_max(woven, sums, 0.0)
                 else:
                     nc.scalar.activation(out=woven, in_=sums, func=ACT.Relu)
@@ -130,7 +148,7 @@ def tile_list_tabres_silu_kernel(tc, tab_words, tab_scales, w1, w2_words, w2_sca
 
         def second_layer(m, c):
             step = m * CHUNKS + c
-            bank = y_banks.tile([P, CHUNK], F32, name="y_bank", tag=f"y{step % 2}")
+            bank = banks.tile([P, CHUNK], F32, name="y_bank", tag=f"bank{step % 2}")
             nc.tensor.matmul_mx(
                 out=bank[:],
                 lhsT=w2_codes[:, 2 * P * m : 2 * P * (m + 1)].bitcast(FP4X4),
@@ -142,11 +160,16 @@ def tile_list_tabres_silu_kernel(tc, tab_words, tab_scales, w1, w2_words, w2_sca
             )
             act = keep.tile([P, CHUNK], F32, name="act", tag=f"act{step % 2}")
             nc.scalar.activation(out=act[:], in_=bank[:], func=ACT.Silu, bias=bias[:, m : m + 1])
-            cols = slice(c * CHUNK, (c + 1) * CHUNK)
-            nc.vector.tensor_tensor(out=result[m][:, cols], in0=resid[m][:].indirect(picks(c)), in1=act[:], op=ADD)
-            if m == ROW_TILES - 1:
-                nc.sync.dma_start(out=out[P * m : P * (m + 1), cols], in_=result[m][:, cols])
-            elif c == CHUNKS - 1:
+            last = step == ROW_TILES * CHUNKS - 1
+            width = CHUNK // 2 if last else CHUNK
+            for lo in range(0, CHUNK, width):
+                first = c * CHUNK + lo
+                cols = slice(first, first + width)
+                picked = resid[m][:].indirect(offsets[:, first // 16 : (first + width) // 16])
+                nc.vector.tensor_tensor(out=result[m][:, cols], in0=picked, in1=act[:, lo : lo + width], op=ADD)
+                if m == ROW_TILES - 1:
+                    nc.sync.dma_start(out=out[P * m : P * (m + 1), cols], in_=result[m][:, cols])
+            if m < ROW_TILES - 1 and c == CHUNKS - 1:
                 nc.sync.dma_start(out=out[P * m : P * (m + 1), :], in_=result[m][:])
 
         for c in range(CHUNKS):

@@ -60,6 +60,8 @@ def tile_list_tabres_silu_kernel(tc, tab_words, tab_scales, w1, w2_words, w2_sca
 
         nc.vector.memset(tab_rows[:].bitcast(I32), 0)
         nc.gpsimd.memset(bias_rows[:], 0.0)
+        warm = keep.tile([P, 1], F32, name="warm")
+        nc.scalar.activation(out=warm[:], in_=bias_rows[:, P - 1 : P], func=ACT.Silu)
         for a in range(PASSES):
             nc.gpsimd.memset(v_plane[a][:].bitcast(I32), 0)
         nc.gpsimd.memset(w2_plane[:].bitcast(I32), 0)

@@ -53,18 +53,18 @@ def tile_list_tabres_silu_kernel(tc, tab_words, tab_scales, w1, w2_words, w2_sca
         v_codes = [[None] * CHUNKS for a in range(PASSES)]
         w1_codes = [keep.tile([P, H], U32, name=f"w1_codes{a}", align_bytes=64) for a in range(PASSES)]
         w1_plane = [None] * PASSES
-        h_bf = [keep.tile([P, PACK * CHUNK], BF16, name=f"h_bf{c}", align_bytes=64) for c in range(CHUNKS)]
-        h_codes = [keep.tile([P, CHUNK], U32, name=f"h_codes{c}", align_bytes=64) for c in range(CHUNKS)]
+        h_bf = [keep.tile([P, PACK * CHUNK], BF16, name=f"h_bf{c}", tag=f"h_bf{c}", align_bytes=64) for c in range(CHUNKS)]
+        h_codes = [None] * CHUNKS
         h_plane = [keep.tile([P, CHUNK], U8, name=f"h_plane{c}", align_bytes=64) for c in range(CHUNKS)]
-        result = [keep.tile([P, S], F32, name=f"result{m}") for m in range(ROW_TILES)]
+        result = [None] * ROW_TILES
 
         nc.vector.memset(tab_rows[:].bitcast(I32), 0)
+        nc.vector.memset(w2_plane[:].bitcast(I32), 0)
         nc.gpsimd.memset(bias_rows[:], 0.0)
         warm = keep.tile([P, 1], F32, name="warm")
         nc.scalar.activation(out=warm[:], in_=bias_rows[:, P - 1 : P], func=ACT.Silu)
         for a in range(PASSES):
             nc.gpsimd.memset(v_plane[a][:].bitcast(I32), 0)
-        nc.gpsimd.memset(w2_plane[:].bitcast(I32), 0)
         make_identity(nc, identity[:])
 
         def load_tab(a):
@@ -98,6 +98,11 @@ def tile_list_tabres_silu_kernel(tc, tab_words, tab_scales, w1, w2_words, w2_sca
         load_w1(0)
         nc.sync.dma_start(offsets[:], offs)
         nc.sync.dma_start(out=tab_rows[0:P:4, :].bitcast(I32), in_=tab_scales.rearrange("a q t -> (a q) t").bitcast(I32))
+        for q in range(QUADS):
+            nc.sync.dma_start(
+                out=w2_plane[32 * q : 32 * q + 4, :].bitcast(I32),
+                in_=w2_scales[0, 4 * q : 4 * q + 4, :].bitcast(I32),
+            )
         load_tab(0)
         load_w1(1)
         nc.sync.dma_start(out=bias_rows[0:ROW_TILES, :], in_=b.rearrange("(m p) -> m p", p=P))
@@ -106,11 +111,6 @@ def tile_list_tabres_silu_kernel(tc, tab_words, tab_scales, w1, w2_words, w2_sca
         load_tab(1)
         place_scale_rows(1)
         nc.sync.dma_start(out=w2_codes[:].bitcast(I32), in_=w2_words[0].bitcast(I32))
-        for q in range(QUADS):
-            nc.sync.dma_start(
-                out=w2_plane[32 * q : 32 * q + 4, :].bitcast(I32),
-                in_=w2_scales[0, 4 * q : 4 * q + 4, :].bitcast(I32),
-            )
         for m in range(ROW_TILES):
             nc.sync.dma_start(out=resid[m][:], in_=rT[P * m : P * (m + 1), :])
 
@@ -124,33 +124,37 @@ def tile_list_tabres_silu_kernel(tc, tab_words, tab_scales, w1, w2_words, w2_sca
         nc.scalar.copy(out=bias[:], in_=bias_bank[:, 0:ROW_TILES])
         quantise_w1(1)
 
-        def first_layer(c):
-            for g in range(CHUNK // GROUP):
-                cols = slice(g * GROUP, (g + 1) * GROUP)
-                group = c * (CHUNK // GROUP) + g
-                bank = banks.tile([P, PACK, GROUP], F32, name="h_bank", tag=f"bank{group if group < 8 else group - 6}")
-                for a in range(PASSES):
-                    for t in range(PACK):
-                        nc.tensor.matmul_mx(
-                            out=bank[:, t, :],
-                            lhsT=w1_codes[a][:, P * t : P * (t + 1)].bitcast(FP8X4),
-                            lhsT_scale=w1_plane[a][:, P * t : P * (t + 1)],
-                            rhs=v_codes[a][c][:, cols].bitcast(FP8X4),
-                            rhs_scale=v_plane[a][4 * a : P, c * CHUNK + g * GROUP : c * CHUNK + (g + 1) * GROUP],
-                            start=(a == 0 and t == 0),
-                            stop=(a == PASSES - 1 and t == PACK - 1),
-                        )
-                woven = h_bf[c][:, PACK * GROUP * g : PACK * GROUP * (g + 1)].rearrange("p (n t) -> p n t", t=PACK)
-                sums = bank[:].rearrange("p t n -> p n t")
-                if c > 0 and g % 2 == 0:
-                    nc.vector.tensor_scalar_max(woven, sums, 0.0)
-                else:
-                    nc.scalar.activation(out=woven, in_=sums, func=ACT.Relu)
-            nc.vector.quantize_mx(out=h_codes[c][:].bitcast(FP8X4), scales=h_plane[c][:], in_=h_bf[c][:])
+        def first_layer(group):
+            c, g = divmod(group, CHUNK // GROUP)
+            cols = slice(g * GROUP, (g + 1) * GROUP)
+            bank = banks.tile([P, PACK, GROUP], F32, name="h_bank", tag=f"bank{group if group < 8 else (1, 5, 7, 0)[group - 8]}")
+            for a in range(PASSES):
+                for t in range(PACK):
+                    nc.tensor.matmul_mx(
+                        out=bank[:, t, :],
+                        lhsT=w1_codes[a][:, P * t : P * (t + 1)].bitcast(FP8X4),
+                        lhsT_scale=w1_plane[a][:, P * t : P * (t + 1)],
+                        rhs=v_codes[a][c][:, cols].bitcast(FP8X4),
+                        rhs_scale=v_plane[a][4 * a : P, group * GROUP : (group + 1) * GROUP],
+                        start=(a == 0 and t == 0),
+                        stop=(a == PASSES - 1 and t == PACK - 1),
+                    )
+            woven = h_bf[c][:, PACK * GROUP * g : PACK * GROUP * (g + 1)].rearrange("p (n t) -> p n t", t=PACK)
+            sums = bank[:].rearrange("p t n -> p n t")
+            if group in (6, 7):
+                nc.vector.tensor_scalar_max(woven, sums, 0.0)
+            else:
+                nc.scalar.activation(out=woven, in_=sums, func=ACT.Relu)
+            if g == CHUNK // GROUP - 1:
+                tag = "act_second" if c == CHUNKS - 1 else f"h_codes{c}"
+                h_codes[c] = keep.tile([P, CHUNK], U32, name=f"h_codes{c}", tag=tag, align_bytes=64)
+                nc.vector.quantize_mx(out=h_codes[c][:].bitcast(FP8X4), scales=h_plane[c][:], in_=h_bf[c][:])
 
-        def second_layer(m, c):
-            step = m * CHUNKS + c
-            bank = banks.tile([P, CHUNK], F32, name="y_bank", tag=f"bank{step % 2}")
+        def second_layer(step, m, c):
+            if c == 0:
+                tag = f"h_bf{CHUNKS - 1}" if m == 1 else f"result{m}"
+                result[m] = keep.tile([P, S], F32, name=f"result{m}", tag=tag, align_bytes=64)
+            bank = banks.tile([P, CHUNK], F32, name="y_bank", tag=f"bank{2 if step == 1 else 0 if step == 0 or step % 2 else 7}")
             nc.tensor.matmul_mx(
                 out=bank[:],
                 lhsT=w2_codes[:, 2 * P * m : 2 * P * (m + 1)].bitcast(FP4X4),
@@ -160,7 +164,7 @@ def tile_list_tabres_silu_kernel(tc, tab_words, tab_scales, w1, w2_words, w2_sca
                 start=True,
                 stop=True,
             )
-            act = keep.tile([P, CHUNK], F32, name="act", tag=f"act{step % 2}")
+            act = keep.tile([P, CHUNK], F32, name="act", tag="act_second" if step == 1 else f"act{step % 2}", align_bytes=64)
             nc.scalar.activation(out=act[:], in_=bank[:], func=ACT.Silu, bias=bias[:, m : m + 1])
             last = step == ROW_TILES * CHUNKS - 1
             width = CHUNK // 2 if last else CHUNK
@@ -176,9 +180,10 @@ def tile_list_tabres_silu_kernel(tc, tab_words, tab_scales, w1, w2_words, w2_sca
 
         for c in range(CHUNKS):
             gather_words(1, c)
-        for c in range(CHUNKS):
-            first_layer(c)
-            second_layer(0, c)
-        for m in range(1, ROW_TILES):
-            for c in range(CHUNKS):
-                second_layer(m, c)
+        early = [(m, c) for m in range(2) for c in range(CHUNKS - 1)]
+        late = [(m, c) for m in range(ROW_TILES) for c in range(CHUNKS) if (m, c) not in early]
+        groups_before = {0: range(0, 8), 1: range(8, 10), 2: range(10, 12)}
+        for step, (m, c) in enumerate(early + late):
+            for group in groups_before.get(step, ()):
+                first_layer(group)
+            second_layer(step, m, c)

@@ -56,15 +56,15 @@ def tile_list_tabres_silu_kernel(tc, tab_words, tab_scales, w1, w2_words, w2_sca
         h_bf = [keep.tile([P, PACK * CHUNK], BF16, name=f"h_bf{c}", tag=f"h_bf{c}", align_bytes=64) for c in range(CHUNKS)]
         h_codes = [None] * CHUNKS
         h_plane = [keep.tile([P, CHUNK], U8, name=f"h_plane{c}", align_bytes=64) for c in range(CHUNKS)]
-        result = [None] * ROW_TILES
+        result_pair = keep.tile([P, 2 * S], F32, name="result_pair")
+        result = [result_pair[:, 0:S], result_pair[:, S : 2 * S]]
+        result += [keep.tile([P, S], F32, name=f"result{m}")[:] for m in range(2, ROW_TILES)]
 
         nc.vector.memset(tab_rows[:].bitcast(I32), 0)
         nc.vector.memset(w2_plane[:].bitcast(I32), 0)
         nc.gpsimd.memset(bias_rows[:], 0.0)
         warm = keep.tile([P, 1], F32, name="warm")
         nc.scalar.activation(out=warm[:], in_=bias_rows[:, P - 1 : P], func=ACT.Silu)
-        for a in range(PASSES):
-            nc.gpsimd.memset(v_plane[a][:].bitcast(I32), 0)
         make_identity(nc, identity[:])
 
         def load_tab(a):
@@ -74,10 +74,11 @@ def tile_list_tabres_silu_kernel(tc, tab_words, tab_scales, w1, w2_words, w2_sca
             nc.sync.dma_start(out=w1_raw[a][:], in_=w1[512 * a : 512 * (a + 1), :].rearrange("(p j) c -> p j c", j=PACK))
 
         def place_scale_rows(a):
-            for r in range(4):
+            nc.vector.tensor_copy(out=v_plane[a][:].bitcast(I32), in_=v_rows[:].bitcast(I32))
+            for r in range(1, 4):
                 nc.sync.dma_start(
                     out=v_plane[a][4 * a + r : P : 32, :].bitcast(I32),
-                    in_=v_rows[64 * a + 4 * r : 64 * (a + 1) : 16, :].bitcast(I32),
+                    in_=v_rows[4 * a + 8 * r : P : 32, :].bitcast(I32),
                 )
 
         def gather_words(a, c):
@@ -97,9 +98,9 @@ def tile_list_tabres_silu_kernel(tc, tab_words, tab_scales, w1, w2_words, w2_sca
 
         load_w1(0)
         nc.sync.dma_start(offsets[:], offs)
-        nc.sync.dma_start(out=tab_rows[0:P:4, :].bitcast(I32), in_=tab_scales.rearrange("a q t -> (a q) t").bitcast(I32))
+        nc.sync.dma_start(out=tab_rows[0:P:4, :].bitcast(I32), in_=tab_scales.rearrange("a q t -> q a t").bitcast(I32))
         for q in range(QUADS):
-            nc.sync.dma_start(
+            nc.gpsimd.dma_start(
                 out=w2_plane[32 * q : 32 * q + 4, :].bitcast(I32),
                 in_=w2_scales[0, 4 * q : 4 * q + 4, :].bitcast(I32),
             )
@@ -151,9 +152,6 @@ def tile_list_tabres_silu_kernel(tc, tab_words, tab_scales, w1, w2_words, w2_sca
                 nc.vector.quantize_mx(out=h_codes[c][:].bitcast(FP8X4), scales=h_plane[c][:], in_=h_bf[c][:])
 
         def second_layer(step, m, c):
-            if c == 0:
-                tag = f"h_bf{CHUNKS - 1}" if m == 1 else f"result{m}"
-                result[m] = keep.tile([P, S], F32, name=f"result{m}", tag=tag, align_bytes=64)
             bank = banks.tile([P, CHUNK], F32, name="y_bank", tag=f"bank{2 if step == 1 else 0 if step == 0 or step % 2 else 7}")
             nc.tensor.matmul_mx(
                 out=bank[:],
@@ -175,8 +173,13 @@ def tile_list_tabres_silu_kernel(tc, tab_words, tab_scales, w1, w2_words, w2_sca
                 nc.vector.tensor_tensor(out=result[m][:, cols], in0=picked, in1=act[:, lo : lo + width], op=ADD)
                 if m == ROW_TILES - 1:
                     nc.sync.dma_start(out=out[P * m : P * (m + 1), cols], in_=result[m][:, cols])
-            if m < ROW_TILES - 1 and c == CHUNKS - 1:
-                nc.sync.dma_start(out=out[P * m : P * (m + 1), :], in_=result[m][:])
+            if m == 1 and c == CHUNKS - 1:
+                nc.sync.dma_start(
+                    out=out[0 : 2 * P, :].rearrange("(m p) s -> p m s", p=P),
+                    in_=result_pair[:].rearrange("p (m s) -> p m s", m=2),
+                )
+            if m == 2 and c == CHUNKS - 1:
+                nc.sync.dma_start(out=out[P * m : P * (m + 1), :], in_=result[m])
 
         for c in range(CHUNKS):
             gather_words(1, c)

@@ -142,12 +142,12 @@ def tile_list_tabres_silu_kernel(tc, tab_words, tab_scales, w1, w2_words, w2_sca
                     )
             woven = h_bf[c][:, PACK * GROUP * g : PACK * GROUP * (g + 1)].rearrange("p (n t) -> p n t", t=PACK)
             sums = bank[:].rearrange("p t n -> p n t")
-            if group in (6, 7):
+            if group in (4, 6, 8):
                 nc.vector.tensor_scalar_max(woven, sums, 0.0)
             else:
                 nc.scalar.activation(out=woven, in_=sums, func=ACT.Relu)
             if g == CHUNK // GROUP - 1:
-                tag = "act_second" if c == CHUNKS - 1 else f"h_codes{c}"
+                tag = "act_first" if c == CHUNKS - 1 else f"h_codes{c}"
                 h_codes[c] = keep.tile([P, CHUNK], U32, name=f"h_codes{c}", tag=tag, align_bytes=64)
                 nc.vector.quantize_mx(out=h_codes[c][:].bitcast(FP8X4), scales=h_plane[c][:], in_=h_bf[c][:])
 
@@ -162,7 +162,7 @@ def tile_list_tabres_silu_kernel(tc, tab_words, tab_scales, w1, w2_words, w2_sca
                 start=True,
                 stop=True,
             )
-            act = keep.tile([P, CHUNK], F32, name="act", tag="act_second" if step == 1 else f"act{step % 2}", align_bytes=64)
+            act = keep.tile([P, CHUNK], F32, name="act", tag=f"act{step % 2}" if step else "act_first", align_bytes=64)
             nc.scalar.activation(out=act[:], in_=bank[:], func=ACT.Silu, bias=bias[:, m : m + 1])
             last = step == ROW_TILES * CHUNKS - 1
             width = CHUNK // 2 if last else CHUNK

@@ -33,32 +33,32 @@ def tile_list_tabres_silu_kernel(tc, tab_words, tab_scales, w1, w2_words, w2_sca
         keep = ctx.enter_context(tc.tile_pool(name="keep", bufs=1))
         banks = ctx.enter_context(tc.psum_pool(name="banks", bufs=1))
 
-        offsets = keep.tile([P, S // 16], U16, name="offsets")
+        offsets = keep.tile([P, S // 16], U16, name="offsets", align_bytes=256)
 
         def picks(c):
             return offsets[:, c * CHUNK // 16 : (c + 1) * CHUNK // 16]
 
-        tab_rows = keep.tile([P, T], U8, name="tab_rows", align_bytes=64)
-        v_rows = keep.tile([P, S], U8, name="v_rows", align_bytes=64)
-        v_plane = [keep.tile([P, S], U8, name=f"v_plane{a}", align_bytes=64) for a in range(PASSES)]
-        tab = [keep.tile([P, T], I32, name=f"tab{a}", tag=f"tab{a}", align_bytes=64) for a in range(PASSES)]
-        w1_raw = [keep.tile([P, PACK, H], F32, name=f"w1_raw{a}") for a in range(PASSES)]
-        resid = [keep.tile([P, T], F32, name=f"resid{m}", align_bytes=64) for m in range(ROW_TILES)]
-        w2_codes = keep.tile([P, 2 * M], U8, name="w2_codes", align_bytes=64)
-        w2_plane = keep.tile([P, M], U8, name="w2_plane", align_bytes=64)
-        bias_rows = keep.tile([P, P], F32, name="bias_rows")
+        tab_rows = keep.tile([P, T], U8, name="tab_rows", align_bytes=256)
+        v_rows = keep.tile([P, S], U8, name="v_rows", align_bytes=256)
+        v_plane = [keep.tile([P, S], U8, name=f"v_plane{a}", align_bytes=256) for a in range(PASSES)]
+        tab = [keep.tile([P, T], I32, name=f"tab{a}", tag=f"tab{a}", align_bytes=256) for a in range(PASSES)]
+        w1_raw = [keep.tile([P, PACK, H], F32, name=f"w1_raw{a}", align_bytes=256) for a in range(PASSES)]
+        resid = [keep.tile([P, T], F32, name=f"resid{m}", align_bytes=256) for m in range(ROW_TILES)]
+        w2_codes = keep.tile([P, 2 * M], U8, name="w2_codes", align_bytes=256)
+        w2_plane = keep.tile([P, M], U8, name="w2_plane", align_bytes=256)
+        bias_rows = keep.tile([P, P], F32, name="bias_rows", align_bytes=256)
         identity = keep.tile([P, P], F32, name="identity")
         bias = keep.tile([P, ROW_TILES], F32, name="bias")
-        w1_bf = [keep.tile([P, PACK * H], BF16, name=f"w1_bf{a}", tag=f"w1_bf{a}", align_bytes=64) for a in range(PASSES)]
+        w1_bf = [keep.tile([P, PACK * H], BF16, name=f"w1_bf{a}", tag=f"w1_bf{a}", align_bytes=256) for a in range(PASSES)]
         v_codes = [[None] * CHUNKS for a in range(PASSES)]
-        w1_codes = [keep.tile([P, H], U32, name=f"w1_codes{a}", align_bytes=64) for a in range(PASSES)]
+        w1_codes = [keep.tile([P, H], U32, name=f"w1_codes{a}", align_bytes=256) for a in range(PASSES)]
         w1_plane = [None] * PASSES
-        h_bf = [keep.tile([P, PACK * CHUNK], BF16, name=f"h_bf{c}", tag=f"h_bf{c}", align_bytes=64) for c in range(CHUNKS)]
+        h_bf = [keep.tile([P, PACK * CHUNK], BF16, name=f"h_bf{c}", tag=f"h_bf{c}", align_bytes=256) for c in range(CHUNKS)]
         h_codes = [None] * CHUNKS
-        h_plane = [keep.tile([P, CHUNK], U8, name=f"h_plane{c}", align_bytes=64) for c in range(CHUNKS)]
-        result_pair = keep.tile([P, 2 * S], F32, name="result_pair")
+        h_plane = [keep.tile([P, CHUNK], U8, name=f"h_plane{c}", align_bytes=256) for c in range(CHUNKS)]
+        result_pair = keep.tile([P, 2 * S], F32, name="result_pair", align_bytes=256)
         result = [result_pair[:, 0:S], result_pair[:, S : 2 * S]]
-        result += [keep.tile([P, S], F32, name=f"result{m}")[:] for m in range(2, ROW_TILES)]
+        result += [keep.tile([P, S], F32, name=f"result{m}", align_bytes=256)[:] for m in range(2, ROW_TILES)]
 
         nc.vector.memset(tab_rows[:].bitcast(I32), 0)
         nc.vector.memset(w2_plane[:].bitcast(I32), 0)
@@ -83,7 +83,7 @@ def tile_list_tabres_silu_kernel(tc, tab_words, tab_scales, w1, w2_words, w2_sca
 
         def gather_words(a, c):
             tag = "w1_bf1" if (a, c) == (1, 0) else f"v_codes{a}_{c}"
-            v_codes[a][c] = keep.tile([P, CHUNK], U32, name=f"v_codes{a}_{c}", tag=tag, align_bytes=64)
+            v_codes[a][c] = keep.tile([P, CHUNK], U32, name=f"v_codes{a}_{c}", tag=tag, align_bytes=256)
             nc.vector.tensor_copy(out=v_codes[a][c][:], in_=tab[a][:].bitcast(U32).indirect(picks(c)))
 
         def round_w1(a):
@@ -93,7 +93,7 @@ def tile_list_tabres_silu_kernel(tc, tab_words, tab_scales, w1, w2_words, w2_sca
             )
 
         def quantise_w1(a):
-            w1_plane[a] = keep.tile([P, H], U8, name=f"w1_plane{a}", tag="tab0" if a == 0 else "w1_plane", align_bytes=64)
+            w1_plane[a] = keep.tile([P, H], U8, name=f"w1_plane{a}", tag="tab0" if a == 0 else "w1_plane", align_bytes=256)
             nc.vector.quantize_mx(out=w1_codes[a][:].bitcast(FP8X4), scales=w1_plane[a][:], in_=w1_bf[a][:])
 
         load_w1(0)
@@ -148,7 +148,7 @@ def tile_list_tabres_silu_kernel(tc, tab_words, tab_scales, w1, w2_words, w2_sca
                 nc.scalar.activation(out=woven, in_=sums, func=ACT.Relu)
             if g == CHUNK // GROUP - 1:
                 tag = "act_first" if c == CHUNKS - 1 else f"h_codes{c}"
-                h_codes[c] = keep.tile([P, CHUNK], U32, name=f"h_codes{c}", tag=tag, align_bytes=64)
+                h_codes[c] = keep.tile([P, CHUNK], U32, name=f"h_codes{c}", tag=tag, align_bytes=256)
                 nc.vector.quantize_mx(out=h_codes[c][:].bitcast(FP8X4), scales=h_plane[c][:], in_=h_bf[c][:])
 
         def second_layer(step, m, c):
@@ -162,7 +162,7 @@ def tile_list_tabres_silu_kernel(tc, tab_words, tab_scales, w1, w2_words, w2_sca
                 start=True,
                 stop=True,
             )
-            act = keep.tile([P, CHUNK], F32, name="act", tag=f"act{step % 2}" if step else "act_first", align_bytes=64)
+            act = keep.tile([P, CHUNK], F32, name="act", tag=f"act{step % 2}" if step else "act_first", align_bytes=256)
             nc.scalar.activation(out=act[:], in_=bank[:], func=ACT.Silu, bias=bias[:, m : m + 1])
             last = step == ROW_TILES * CHUNKS - 1
             width = CHUNK // 2 if last else CHUNK

@@ -24,7 +24,6 @@ CHUNK = 512
 CHUNKS = S // CHUNK
 GROUP = CHUNK // PACK
 ROW_TILES = M // P
-QUADS = 4
 
 
 def tile_list_tabres_silu_kernel(tc, tab_words, tab_scales, w1, w2_words, w2_scales, rT, b, offs, out):
@@ -40,12 +39,12 @@ def tile_list_tabres_silu_kernel(tc, tab_words, tab_scales, w1, w2_words, w2_sca
 
         tab_rows = keep.tile([P, T], U8, name="tab_rows", align_bytes=256)
         v_rows = keep.tile([P, S], U8, name="v_rows", align_bytes=256)
-        v_plane = [keep.tile([P, S], U8, name=f"v_plane{a}", align_bytes=256) for a in range(PASSES)]
+        v_plane = [keep.tile([P, S + (M if a == 0 else 0)], U8, name=f"v_plane{a}", align_bytes=256) for a in range(PASSES)]
         tab = [keep.tile([P, T], I32, name=f"tab{a}", tag=f"tab{a}", align_bytes=256) for a in range(PASSES)]
         w1_raw = [keep.tile([P, PACK, H], F32, name=f"w1_raw{a}", align_bytes=256) for a in range(PASSES)]
         resid = [keep.tile([P, T], F32, name=f"resid{m}", align_bytes=256) for m in range(ROW_TILES)]
         w2_codes = keep.tile([P, 2 * M], U8, name="w2_codes", align_bytes=256)
-        w2_plane = keep.tile([P, M], U8, name="w2_plane", align_bytes=256)
+        w2_plane = v_plane[0][:, S : S + M]
         bias_rows = keep.tile([P, P], F32, name="bias_rows", align_bytes=256)
         identity = keep.tile([P, P], F32, name="identity")
         bias = keep.tile([P, ROW_TILES], F32, name="bias")
@@ -61,7 +60,7 @@ def tile_list_tabres_silu_kernel(tc, tab_words, tab_scales, w1, w2_words, w2_sca
         result += [keep.tile([P, S], F32, name=f"result{m}", align_bytes=256)[:] for m in range(2, ROW_TILES)]
 
         nc.vector.memset(tab_rows[:].bitcast(I32), 0)
-        nc.vector.memset(w2_plane[:].bitcast(I32), 0)
+        nc.vector.memset(w2_plane.bitcast(I32), 0)
         nc.gpsimd.memset(bias_rows[:], 0.0)
         warm = keep.tile([P, 1], F32, name="warm")
         nc.scalar.activation(out=warm[:], in_=bias_rows[:, P - 1 : P], func=ACT.Silu)
@@ -74,15 +73,15 @@ def tile_list_tabres_silu_kernel(tc, tab_words, tab_scales, w1, w2_words, w2_sca
             nc.sync.dma_start(out=w1_raw[a][:], in_=w1[512 * a : 512 * (a + 1), :].rearrange("(p j) c -> p j c", j=PACK))
 
         def place_scale_rows(a):
-            nc.vector.tensor_copy(out=v_plane[a][:].bitcast(I32), in_=v_rows[:].bitcast(I32))
+            nc.vector.tensor_copy(out=v_plane[a][:, 0:S].bitcast(I32), in_=v_rows[:].bitcast(I32))
             for r in range(1, 4):
                 nc.sync.dma_start(
                     out=v_plane[a][4 * a + r : P : 32, :].bitcast(I32),
-                    in_=v_rows[4 * a + 8 * r : P : 32, :].bitcast(I32),
+                    in_=v_plane[a][4 * a + 8 * r : P : 32, :].bitcast(I32),
                 )
 
         def gather_words(a, c):
-            tag = "w1_bf1" if (a, c) == (1, 0) else f"v_codes{a}_{c}"
+            tag = "w1_bf0" if (a, c) == (0, 0) else f"v_codes{a}_{c}"
             v_codes[a][c] = keep.tile([P, CHUNK], U32, name=f"v_codes{a}_{c}", tag=tag, align_bytes=256)
             nc.vector.tensor_copy(out=v_codes[a][c][:], in_=tab[a][:].bitcast(U32).indirect(picks(c)))
 
@@ -93,43 +92,39 @@ def tile_list_tabres_silu_kernel(tc, tab_words, tab_scales, w1, w2_words, w2_sca
             )
 
         def quantise_w1(a):
-            w1_plane[a] = keep.tile([P, H], U8, name=f"w1_plane{a}", tag="tab0" if a == 0 else "w1_plane", align_bytes=256)
+            w1_plane[a] = keep.tile([P, H], U8, name=f"w1_plane{a}", tag="tab1" if a == 1 else "w1_plane", align_bytes=256)
             nc.vector.quantize_mx(out=w1_codes[a][:].bitcast(FP8X4), scales=w1_plane[a][:], in_=w1_bf[a][:])
 
-        load_w1(0)
+        load_w1(1)
         nc.sync.dma_start(offsets[:], offs)
         nc.sync.dma_start(out=tab_rows[0:P:4, :].bitcast(I32), in_=tab_scales.rearrange("a q t -> q a t").bitcast(I32))
-        for q in range(QUADS):
-            nc.gpsimd.dma_start(
-                out=w2_plane[32 * q : 32 * q + 4, :].bitcast(I32),
-                in_=w2_scales[0, 4 * q : 4 * q + 4, :].bitcast(I32),
-            )
-        load_tab(0)
-        load_w1(1)
-        nc.sync.dma_start(out=bias_rows[0:ROW_TILES, :], in_=b.rearrange("(m p) -> m p", p=P))
-        nc.vector.tensor_copy(out=v_rows[:], in_=tab_rows[:].indirect(offsets[:]))
-        place_scale_rows(0)
         load_tab(1)
+        load_w1(0)
+        nc.sync.dma_start(out=v_plane[0][0:P:8, S : S + M].bitcast(I32), in_=w2_scales[0].bitcast(I32))
+        nc.gpsimd.dma_start(out=bias_rows[0:ROW_TILES, :], in_=b.rearrange("(m p) -> m p", p=P))
+        nc.vector.tensor_copy(out=v_rows[:], in_=tab_rows[:].indirect(offsets[:]))
         place_scale_rows(1)
+        load_tab(0)
+        place_scale_rows(0)
         nc.sync.dma_start(out=w2_codes[:].bitcast(I32), in_=w2_words[0].bitcast(I32))
         for m in range(ROW_TILES):
             nc.sync.dma_start(out=resid[m][:], in_=rT[P * m : P * (m + 1), :])
 
-        round_w1(0)
-        for c in range(CHUNKS):
-            gather_words(0, c)
-        quantise_w1(0)
         round_w1(1)
+        for c in range(CHUNKS):
+            gather_words(1, c)
+        quantise_w1(1)
+        round_w1(0)
         bias_bank = banks.tile([P, P], F32, name="bias_bank", tag="bank7")
         nc.tensor.transpose(bias_bank[:], bias_rows[:], identity[:])
         nc.scalar.copy(out=bias[:], in_=bias_bank[:, 0:ROW_TILES])
-        quantise_w1(1)
+        quantise_w1(0)
 
         def first_layer(group):
             c, g = divmod(group, CHUNK // GROUP)
             cols = slice(g * GROUP, (g + 1) * GROUP)
             bank = banks.tile([P, PACK, GROUP], F32, name="h_bank", tag=f"bank{group if group < 8 else (1, 5, 7, 0)[group - 8]}")
-            for a in range(PASSES):
+            for a in (1, 0):
                 for t in range(PACK):
                     nc.tensor.matmul_mx(
                         out=bank[:, t, :],
@@ -137,12 +132,12 @@ def tile_list_tabres_silu_kernel(tc, tab_words, tab_scales, w1, w2_words, w2_sca
                         lhsT_scale=w1_plane[a][:, P * t : P * (t + 1)],
                         rhs=v_codes[a][c][:, cols].bitcast(FP8X4),
                         rhs_scale=v_plane[a][4 * a : P, group * GROUP : (group + 1) * GROUP],
-                        start=(a == 0 and t == 0),
-                        stop=(a == PASSES - 1 and t == PACK - 1),
+                        start=(a == 1 and t == 0),
+                        stop=(a == 0 and t == PACK - 1),
                     )
             woven = h_bf[c][:, PACK * GROUP * g : PACK * GROUP * (g + 1)].rearrange("p (n t) -> p n t", t=PACK)
             sums = bank[:].rearrange("p t n -> p n t")
-            if group in (4, 6, 8):
+            if group in (4, 6):
                 nc.vector.tensor_scalar_max(woven, sums, 0.0)
             else:
                 nc.scalar.activation(out=woven, in_=sums, func=ACT.Relu)
@@ -151,26 +146,33 @@ def tile_list_tabres_silu_kernel(tc, tab_words, tab_scales, w1, w2_words, w2_sca
                 h_codes[c] = keep.tile([P, CHUNK], U32, name=f"h_codes{c}", tag=tag, align_bytes=256)
                 nc.vector.quantize_mx(out=h_codes[c][:].bitcast(FP8X4), scales=h_plane[c][:], in_=h_bf[c][:])
 
+        act_row = {}
+        sums_after = {(2, 0): (), (2, 1): (), (2, 2): ((0, S),), (3, 2): ((1024, 384), (1408, 128))}
+
         def second_layer(step, m, c):
-            bank = banks.tile([P, CHUNK], F32, name="y_bank", tag=f"bank{2 if step == 1 else 0 if step == 0 or step % 2 else 7}")
+            bank = banks.tile([P, CHUNK], F32, name="y_bank", tag=f"bank{(0, 2, 7, 0, 5, 1, 2, 7, 0, 5, 1, 2)[step]}")
             nc.tensor.matmul_mx(
                 out=bank[:],
                 lhsT=w2_codes[:, 2 * P * m : 2 * P * (m + 1)].bitcast(FP4X4),
-                lhsT_scale=w2_plane[:, P * m : P * (m + 1)],
+                lhsT_scale=v_plane[0][:, S + P * m : S + P * (m + 1)],
                 rhs=h_codes[c][:].bitcast(FP8X4),
                 rhs_scale=h_plane[c][:],
                 start=True,
                 stop=True,
             )
-            act = keep.tile([P, CHUNK], F32, name="act", tag=f"act{step % 2}" if step else "act_first", align_bytes=256)
-            nc.scalar.activation(out=act[:], in_=bank[:], func=ACT.Silu, bias=bias[:, m : m + 1])
-            last = step == ROW_TILES * CHUNKS - 1
-            width = CHUNK // 2 if last else CHUNK
-            for lo in range(0, CHUNK, width):
-                first = c * CHUNK + lo
+            if m < 2:
+                act_tile = keep.tile([P, CHUNK], F32, name="act", tag=("act_first", "act1", "act0", "act1", "act0", "act2")[step], align_bytes=256)
+                act, base = act_tile[:], c * CHUNK
+                nc.scalar.activation(out=act, in_=bank[:], func=ACT.Silu, bias=bias[:, m : m + 1])
+            else:
+                if c == 0:
+                    act_row[m] = keep.tile([P, S], F32, name="act_row", tag="act1" if m == 2 else "act0", align_bytes=256)
+                act, base = act_row[m][:], 0
+                nc.scalar.activation(out=act[:, c * CHUNK : (c + 1) * CHUNK], in_=bank[:], func=ACT.Silu, bias=bias[:, m : m + 1])
+            for first, width in sums_after.get((m, c), ((c * CHUNK, CHUNK),)):
                 cols = slice(first, first + width)
                 picked = resid[m][:].indirect(offsets[:, first // 16 : (first + width) // 16])
-                nc.vector.tensor_tensor(out=result[m][:, cols], in0=picked, in1=act[:, lo : lo + width], op=ADD)
+                nc.vector.tensor_tensor(out=result[m][:, cols], in0=picked, in1=act[:, first - base : first - base + width], op=ADD)
                 if m == ROW_TILES - 1:
                     nc.sync.dma_start(out=out[P * m : P * (m + 1), cols], in_=result[m][:, cols])
             if m == 1 and c == CHUNKS - 1:
@@ -182,7 +184,7 @@ def tile_list_tabres_silu_kernel(tc, tab_words, tab_scales, w1, w2_words, w2_sca
                 nc.sync.dma_start(out=out[P * m : P * (m + 1), :], in_=result[m])
 
         for c in range(CHUNKS):
-            gather_words(1, c)
+            gather_words(0, c)
         early = [(m, c) for m in range(2) for c in range(CHUNKS - 1)]
         late = [(m, c) for m in range(ROW_TILES) for c in range(CHUNKS) if (m, c) not in early]
         groups_before = {0: range(0, 8), 1: range(8, 10), 2: range(10, 12)}

@@ -101,7 +101,7 @@ def tile_list_tabres_silu_kernel(tc, tab_words, tab_scales, w1, w2_words, w2_sca
         load_tab(1)
         load_w1(0)
         nc.sync.dma_start(out=v_plane[0][0:P:8, S : S + M].bitcast(I32), in_=w2_scales[0].bitcast(I32))
-        nc.gpsimd.dma_start(out=bias_rows[0:ROW_TILES, :], in_=b.rearrange("(m p) -> m p", p=P))
+        nc.sync.dma_start(out=bias_rows[0:ROW_TILES, :], in_=b.rearrange("(m p) -> m p", p=P))
         nc.vector.tensor_copy(out=v_rows[:], in_=tab_rows[:].indirect(offsets[:]))
         place_scale_rows(1)
         load_tab(0)
@@ -147,7 +147,7 @@ def tile_list_tabres_silu_kernel(tc, tab_words, tab_scales, w1, w2_words, w2_sca
                 nc.vector.quantize_mx(out=h_codes[c][:].bitcast(FP8X4), scales=h_plane[c][:], in_=h_bf[c][:])
 
         act_row = {}
-        sums_after = {(2, 0): (), (2, 1): (), (2, 2): ((0, S),), (3, 2): ((1024, 384), (1408, 128))}
+        sums_after = {(2, 0): (), (2, 1): (), (2, 2): ((0, S),), (3, 0): (), (3, 1): ((0, 896),), (3, 2): ((896, 448), (1344, 192))}
 
         def second_layer(step, m, c):
             bank = banks.tile([P, CHUNK], F32, name="y_bank", tag=f"bank{(0, 2, 7, 0, 5, 1, 2, 7, 0, 5, 1, 2)[step]}")

@@ -92,16 +92,18 @@ def tile_list_tabres_silu_kernel(tc, tab_words, tab_scales, w1, w2_words, w2_sca
             )
 
         def quantise_w1(a):
-            w1_plane[a] = keep.tile([P, H], U8, name=f"w1_plane{a}", tag="tab1" if a == 1 else "w1_plane", align_bytes=256)
+            w1_plane[a] = keep.tile([P, H], U8, name=f"w1_plane{a}", tag=f"w1_plane{a}", align_bytes=256)
             nc.vector.quantize_mx(out=w1_codes[a][:].bitcast(FP8X4), scales=w1_plane[a][:], in_=w1_bf[a][:])
 
-        load_w1(1)
+        w1_first = w1[512:1024, :].rearrange("(p j) c -> p j c", j=PACK)
+        nc.sync.dma_start(out=w1_raw[1][:, 0:3, :], in_=w1_first[:, 0:3, :])
         nc.sync.dma_start(offsets[:], offs)
         nc.sync.dma_start(out=tab_rows[0:P:4, :].bitcast(I32), in_=tab_scales.rearrange("a q t -> q a t").bitcast(I32))
+        nc.sync.dma_start(out=w1_raw[1][:, 3:4, :], in_=w1_first[:, 3:4, :])
         load_tab(1)
         load_w1(0)
         nc.sync.dma_start(out=v_plane[0][0:P:8, S : S + M].bitcast(I32), in_=w2_scales[0].bitcast(I32))
-        nc.sync.dma_start(out=bias_rows[0:ROW_TILES, :], in_=b.rearrange("(m p) -> m p", p=P))
+        nc.gpsimd.dma_start(out=bias_rows[0:ROW_TILES, :], in_=b.rearrange("(m p) -> m p", p=P))
         nc.vector.tensor_copy(out=v_rows[:], in_=tab_rows[:].indirect(offsets[:]))
         place_scale_rows(1)
         load_tab(0)

@@ -19,11 +19,22 @@ ADD = mybir.AluOpType.add
 
 P = 128
 PACK = 4
-PASSES = K // (P * PACK)
+PASS_ROWS = P * PACK
+PASSES = K // PASS_ROWS
 CHUNK = 512
 CHUNKS = S // CHUNK
 GROUP = CHUNK // PACK
+GROUPS_PER_CHUNK = CHUNK // GROUP
 ROW_TILES = M // P
+PER_COLUMN = 16
+QUADRANT = 32
+BANKS = 8
+ALIGN = 256
+
+EARLY_PASS, LATE_PASS = 1, 0
+W1_LEAD = 3
+VECTOR_RELUS = (4, 6)
+LAST_PIECES = (896, 448, 192)
 
 
 def tile_list_tabres_silu_kernel(tc, tab_words, tab_scales, w1, w2_words, w2_scales, rT, b, offs, out):
@@ -32,32 +43,32 @@ def tile_list_tabres_silu_kernel(tc, tab_words, tab_scales, w1, w2_words, w2_sca
         keep = ctx.enter_context(tc.tile_pool(name="keep", bufs=1))
         banks = ctx.enter_context(tc.psum_pool(name="banks", bufs=1))
 
-        offsets = keep.tile([P, S // 16], U16, name="offsets", align_bytes=256)
+        offsets = keep.tile([P, S // PER_COLUMN], U16, name="offsets", align_bytes=ALIGN)
 
-        def picks(c):
-            return offsets[:, c * CHUNK // 16 : (c + 1) * CHUNK // 16]
+        def picks(first, count):
+            return offsets[:, first // PER_COLUMN : (first + count) // PER_COLUMN]
 
-        tab_rows = keep.tile([P, T], U8, name="tab_rows", align_bytes=256)
-        v_rows = keep.tile([P, S], U8, name="v_rows", align_bytes=256)
-        v_plane = [keep.tile([P, S + (M if a == 0 else 0)], U8, name=f"v_plane{a}", align_bytes=256) for a in range(PASSES)]
-        tab = [keep.tile([P, T], I32, name=f"tab{a}", tag=f"tab{a}", align_bytes=256) for a in range(PASSES)]
-        w1_raw = [keep.tile([P, PACK, H], F32, name=f"w1_raw{a}", align_bytes=256) for a in range(PASSES)]
-        resid = [keep.tile([P, T], F32, name=f"resid{m}", align_bytes=256) for m in range(ROW_TILES)]
-        w2_codes = keep.tile([P, 2 * M], U8, name="w2_codes", align_bytes=256)
-        w2_plane = v_plane[0][:, S : S + M]
-        bias_rows = keep.tile([P, P], F32, name="bias_rows", align_bytes=256)
+        tab_rows = keep.tile([P, T], U8, name="tab_rows", align_bytes=ALIGN)
+        v_rows = keep.tile([P, S], U8, name="v_rows", align_bytes=ALIGN)
+        v_plane = [keep.tile([P, S + (M if a == LATE_PASS else 0)], U8, name=f"v_plane{a}", align_bytes=ALIGN) for a in range(PASSES)]
+        tab = [keep.tile([P, T], I32, name=f"tab{a}", align_bytes=ALIGN) for a in range(PASSES)]
+        w1_raw = [keep.tile([P, PACK, H], F32, name=f"w1_raw{a}", align_bytes=ALIGN) for a in range(PASSES)]
+        resid = [keep.tile([P, T], F32, name=f"resid{m}", align_bytes=ALIGN) for m in range(ROW_TILES)]
+        w2_codes = keep.tile([P, 2 * M], U8, name="w2_codes", align_bytes=ALIGN)
+        w2_plane = v_plane[LATE_PASS][:, S : S + M]
+        bias_rows = keep.tile([P, P], F32, name="bias_rows", align_bytes=ALIGN)
         identity = keep.tile([P, P], F32, name="identity")
         bias = keep.tile([P, ROW_TILES], F32, name="bias")
-        w1_bf = [keep.tile([P, PACK * H], BF16, name=f"w1_bf{a}", tag=f"w1_bf{a}", align_bytes=256) for a in range(PASSES)]
+        w1_bf = [keep.tile([P, PACK * H], BF16, name=f"w1_bf{a}", align_bytes=ALIGN) for a in range(PASSES)]
         v_codes = [[None] * CHUNKS for a in range(PASSES)]
-        w1_codes = [keep.tile([P, H], U32, name=f"w1_codes{a}", align_bytes=256) for a in range(PASSES)]
+        w1_codes = [keep.tile([P, H], U32, name=f"w1_codes{a}", align_bytes=ALIGN) for a in range(PASSES)]
         w1_plane = [None] * PASSES
-        h_bf = [keep.tile([P, PACK * CHUNK], BF16, name=f"h_bf{c}", tag=f"h_bf{c}", align_bytes=256) for c in range(CHUNKS)]
+        h_bf = [keep.tile([P, PACK * CHUNK], BF16, name=f"h_bf{c}", align_bytes=ALIGN) for c in range(CHUNKS)]
         h_codes = [None] * CHUNKS
-        h_plane = [keep.tile([P, CHUNK], U8, name=f"h_plane{c}", align_bytes=256) for c in range(CHUNKS)]
-        result_pair = keep.tile([P, 2 * S], F32, name="result_pair", align_bytes=256)
+        h_plane = [keep.tile([P, CHUNK], U8, name=f"h_plane{c}", align_bytes=ALIGN) for c in range(CHUNKS)]
+        result_pair = keep.tile([P, 2 * S], F32, name="result_pair", align_bytes=ALIGN)
         result = [result_pair[:, 0:S], result_pair[:, S : 2 * S]]
-        result += [keep.tile([P, S], F32, name=f"result{m}", align_bytes=256)[:] for m in range(2, ROW_TILES)]
+        result += [keep.tile([P, S], F32, name=f"result{m}", align_bytes=ALIGN)[:] for m in range(2, ROW_TILES)]
 
         nc.vector.memset(tab_rows[:].bitcast(I32), 0)
         nc.vector.memset(w2_plane.bitcast(I32), 0)
@@ -66,67 +77,69 @@ def tile_list_tabres_silu_kernel(tc, tab_words, tab_scales, w1, w2_words, w2_sca
         nc.scalar.activation(out=warm[:], in_=bias_rows[:, P - 1 : P], func=ACT.Silu)
         make_identity(nc, identity[:])
 
+        def w1_rows(a):
+            return w1[PASS_ROWS * a : PASS_ROWS * (a + 1), :].rearrange("(p j) c -> p j c", j=PACK)
+
         def load_tab(a):
             nc.sync.dma_start(out=tab[a][:], in_=tab_words[a].rearrange("p t i -> p (t i)").bitcast(I32))
 
-        def load_w1(a):
-            nc.sync.dma_start(out=w1_raw[a][:], in_=w1[512 * a : 512 * (a + 1), :].rearrange("(p j) c -> p j c", j=PACK))
-
         def place_scale_rows(a):
             nc.vector.tensor_copy(out=v_plane[a][:, 0:S].bitcast(I32), in_=v_rows[:].bitcast(I32))
-            for r in range(1, 4):
+            for row in range(1, 4):
                 nc.sync.dma_start(
-                    out=v_plane[a][4 * a + r : P : 32, :].bitcast(I32),
-                    in_=v_plane[a][4 * a + 8 * r : P : 32, :].bitcast(I32),
+                    out=v_plane[a][4 * a + row : P : QUADRANT, :].bitcast(I32),
+                    in_=v_plane[a][4 * a + 8 * row : P : QUADRANT, :].bitcast(I32),
                 )
 
         def gather_words(a, c):
-            tag = "w1_bf0" if (a, c) == (0, 0) else f"v_codes{a}_{c}"
-            v_codes[a][c] = keep.tile([P, CHUNK], U32, name=f"v_codes{a}_{c}", tag=tag, align_bytes=256)
-            nc.vector.tensor_copy(out=v_codes[a][c][:], in_=tab[a][:].bitcast(U32).indirect(picks(c)))
+            v_codes[a][c] = keep.tile([P, CHUNK], U32, name=f"v_codes{a}_{c}", align_bytes=ALIGN)
+            nc.vector.tensor_copy(out=v_codes[a][c][:], in_=tab[a][:].bitcast(U32).indirect(picks(c * CHUNK, CHUNK)))
 
         def round_w1(a):
             nc.scalar.copy(
-                out=w1_bf[a][:].rearrange("p (t m j) -> p m t j", t=PACK, j=PACK),
-                in_=w1_raw[a][:].rearrange("p j (m t) -> p m t j", t=PACK),
+                out=w1_bf[a][:].rearrange("p (t i j) -> p i t j", t=PACK, j=PACK),
+                in_=w1_raw[a][:].rearrange("p j (i t) -> p i t j", t=PACK),
             )
 
         def quantise_w1(a):
-            w1_plane[a] = keep.tile([P, H], U8, name=f"w1_plane{a}", tag=f"w1_plane{a}", align_bytes=256)
+            w1_plane[a] = keep.tile([P, H], U8, name=f"w1_plane{a}", align_bytes=ALIGN)
             nc.vector.quantize_mx(out=w1_codes[a][:].bitcast(FP8X4), scales=w1_plane[a][:], in_=w1_bf[a][:])
 
-        w1_first = w1[512:1024, :].rearrange("(p j) c -> p j c", j=PACK)
-        nc.sync.dma_start(out=w1_raw[1][:, 0:3, :], in_=w1_first[:, 0:3, :])
+        nc.sync.dma_start(out=w1_raw[EARLY_PASS][:, 0:W1_LEAD, :], in_=w1_rows(EARLY_PASS)[:, 0:W1_LEAD, :])
         nc.sync.dma_start(offsets[:], offs)
         nc.sync.dma_start(out=tab_rows[0:P:4, :].bitcast(I32), in_=tab_scales.rearrange("a q t -> q a t").bitcast(I32))
-        nc.sync.dma_start(out=w1_raw[1][:, 3:4, :], in_=w1_first[:, 3:4, :])
-        load_tab(1)
-        load_w1(0)
-        nc.sync.dma_start(out=v_plane[0][0:P:8, S : S + M].bitcast(I32), in_=w2_scales[0].bitcast(I32))
+        nc.sync.dma_start(out=w1_raw[EARLY_PASS][:, W1_LEAD:PACK, :], in_=w1_rows(EARLY_PASS)[:, W1_LEAD:PACK, :])
+        nc.sync.dma_start(out=w1_raw[LATE_PASS][:], in_=w1_rows(LATE_PASS))
+        load_tab(EARLY_PASS)
+        nc.sync.dma_start(out=v_plane[LATE_PASS][0:P:8, S : S + M].bitcast(I32), in_=w2_scales[0].bitcast(I32))
         nc.gpsimd.dma_start(out=bias_rows[0:ROW_TILES, :], in_=b.rearrange("(m p) -> m p", p=P))
         nc.vector.tensor_copy(out=v_rows[:], in_=tab_rows[:].indirect(offsets[:]))
-        place_scale_rows(1)
-        load_tab(0)
-        place_scale_rows(0)
+        place_scale_rows(EARLY_PASS)
+        load_tab(LATE_PASS)
+        place_scale_rows(LATE_PASS)
         nc.sync.dma_start(out=w2_codes[:].bitcast(I32), in_=w2_words[0].bitcast(I32))
         for m in range(ROW_TILES):
             nc.sync.dma_start(out=resid[m][:], in_=rT[P * m : P * (m + 1), :])
 
-        round_w1(1)
-        for c in range(CHUNKS):
-            gather_words(1, c)
-        quantise_w1(1)
-        round_w1(0)
-        bias_bank = banks.tile([P, P], F32, name="bias_bank", tag="bank7")
+        round_w1(EARLY_PASS)
+        quantise_w1(EARLY_PASS)
+        round_w1(LATE_PASS)
+        bias_bank = banks.tile([P, P], F32, name="bias_bank", tag=f"bank{BANKS - 1}")
         nc.tensor.transpose(bias_bank[:], bias_rows[:], identity[:])
         nc.scalar.copy(out=bias[:], in_=bias_bank[:, 0:ROW_TILES])
-        quantise_w1(0)
+        quantise_w1(LATE_PASS)
+        for c in range(CHUNKS):
+            gather_words(EARLY_PASS, c)
+
+        h_bank_of = list(range(BANKS)) + [1, 5, 7, 0]
+        y_rotation = (2, 7, 0, 5, 1)
+        silu_slot_of = ("slot_first", "slot_b", "slot_a", "slot_b", "slot_a", "slot_sixth")
 
         def first_layer(group):
-            c, g = divmod(group, CHUNK // GROUP)
+            c, g = divmod(group, GROUPS_PER_CHUNK)
             cols = slice(g * GROUP, (g + 1) * GROUP)
-            bank = banks.tile([P, PACK, GROUP], F32, name="h_bank", tag=f"bank{group if group < 8 else (1, 5, 7, 0)[group - 8]}")
-            for a in (1, 0):
+            bank = banks.tile([P, PACK, GROUP], F32, name="h_bank", tag=f"bank{h_bank_of[group]}")
+            for a in (EARLY_PASS, LATE_PASS):
                 for t in range(PACK):
                     nc.tensor.matmul_mx(
                         out=bank[:, t, :],
@@ -134,63 +147,65 @@ def tile_list_tabres_silu_kernel(tc, tab_words, tab_scales, w1, w2_words, w2_sca
                         lhsT_scale=w1_plane[a][:, P * t : P * (t + 1)],
                         rhs=v_codes[a][c][:, cols].bitcast(FP8X4),
                         rhs_scale=v_plane[a][4 * a : P, group * GROUP : (group + 1) * GROUP],
-                        start=(a == 1 and t == 0),
-                        stop=(a == 0 and t == PACK - 1),
+                        start=(a == EARLY_PASS and t == 0),
+                        stop=(a == LATE_PASS and t == PACK - 1),
                     )
             woven = h_bf[c][:, PACK * GROUP * g : PACK * GROUP * (g + 1)].rearrange("p (n t) -> p n t", t=PACK)
             sums = bank[:].rearrange("p t n -> p n t")
-            if group in (4, 6):
+            if group in VECTOR_RELUS:
                 nc.vector.tensor_scalar_max(woven, sums, 0.0)
             else:
                 nc.scalar.activation(out=woven, in_=sums, func=ACT.Relu)
-            if g == CHUNK // GROUP - 1:
-                tag = "act_first" if c == CHUNKS - 1 else f"h_codes{c}"
-                h_codes[c] = keep.tile([P, CHUNK], U32, name=f"h_codes{c}", tag=tag, align_bytes=256)
+            if g == GROUPS_PER_CHUNK - 1:
+                tag = silu_slot_of[0] if c == CHUNKS - 1 else f"h_codes{c}"
+                h_codes[c] = keep.tile([P, CHUNK], U32, name=f"h_codes{c}", tag=tag, align_bytes=ALIGN)
                 nc.vector.quantize_mx(out=h_codes[c][:].bitcast(FP8X4), scales=h_plane[c][:], in_=h_bf[c][:])
 
-        act_row = {}
-        sums_after = {(2, 0): (), (2, 1): (), (2, 2): ((0, S),), (3, 0): (), (3, 1): ((0, 896),), (3, 2): ((896, 448), (1344, 192))}
-
-        def second_layer(step, m, c):
-            bank = banks.tile([P, CHUNK], F32, name="y_bank", tag=f"bank{(0, 2, 7, 0, 5, 1, 2, 7, 0, 5, 1, 2)[step]}")
+        def second_product(step, m, c):
+            bank = banks.tile([P, CHUNK], F32, name="y_bank", tag=f"bank{y_rotation[(step - 1) % len(y_rotation)] if step else 0}")
             nc.tensor.matmul_mx(
                 out=bank[:],
                 lhsT=w2_codes[:, 2 * P * m : 2 * P * (m + 1)].bitcast(FP4X4),
-                lhsT_scale=v_plane[0][:, S + P * m : S + P * (m + 1)],
+                lhsT_scale=v_plane[LATE_PASS][:, S + P * m : S + P * (m + 1)],
                 rhs=h_codes[c][:].bitcast(FP8X4),
                 rhs_scale=h_plane[c][:],
                 start=True,
                 stop=True,
             )
-            if m < 2:
-                act_tile = keep.tile([P, CHUNK], F32, name="act", tag=("act_first", "act1", "act0", "act1", "act0", "act2")[step], align_bytes=256)
-                act, base = act_tile[:], c * CHUNK
-                nc.scalar.activation(out=act, in_=bank[:], func=ACT.Silu, bias=bias[:, m : m + 1])
-            else:
-                if c == 0:
-                    act_row[m] = keep.tile([P, S], F32, name="act_row", tag="act1" if m == 2 else "act0", align_bytes=256)
-                act, base = act_row[m][:], 0
-                nc.scalar.activation(out=act[:, c * CHUNK : (c + 1) * CHUNK], in_=bank[:], func=ACT.Silu, bias=bias[:, m : m + 1])
-            for first, width in sums_after.get((m, c), ((c * CHUNK, CHUNK),)):
-                cols = slice(first, first + width)
-                picked = resid[m][:].indirect(offsets[:, first // 16 : (first + width) // 16])
-                nc.vector.tensor_tensor(out=result[m][:, cols], in0=picked, in1=act[:, first - base : first - base + width], op=ADD)
-                if m == ROW_TILES - 1:
-                    nc.sync.dma_start(out=out[P * m : P * (m + 1), cols], in_=result[m][:, cols])
-            if m == 1 and c == CHUNKS - 1:
-                nc.sync.dma_start(
-                    out=out[0 : 2 * P, :].rearrange("(m p) s -> p m s", p=P),
-                    in_=result_pair[:].rearrange("p (m s) -> p m s", m=2),
-                )
-            if m == 2 and c == CHUNKS - 1:
-                nc.sync.dma_start(out=out[P * m : P * (m + 1), :], in_=result[m])
+            return bank
+
+        def silu(dest, bank, m):
+            nc.scalar.activation(out=dest, in_=bank[:], func=ACT.Silu, bias=bias[:, m : m + 1])
+
+        def add_residual(m, first, count, activated):
+            picked = resid[m][:].indirect(picks(first, count))
+            nc.vector.tensor_tensor(out=result[m][:, first : first + count], in0=picked, in1=activated, op=ADD)
 
         for c in range(CHUNKS):
-            gather_words(0, c)
-        early = [(m, c) for m in range(2) for c in range(CHUNKS - 1)]
-        late = [(m, c) for m in range(ROW_TILES) for c in range(CHUNKS) if (m, c) not in early]
+            gather_words(LATE_PASS, c)
+
+        pair_steps = [(m, c) for m in range(2) for c in range(CHUNKS - 1)] + [(m, CHUNKS - 1) for m in range(2)]
         groups_before = {0: range(0, 8), 1: range(8, 10), 2: range(10, 12)}
-        for step, (m, c) in enumerate(early + late):
+        for step, (m, c) in enumerate(pair_steps):
             for group in groups_before.get(step, ()):
                 first_layer(group)
-            second_layer(step, m, c)
+            bank = second_product(step, m, c)
+            activated = keep.tile([P, CHUNK], F32, name="activated", tag=silu_slot_of[step], align_bytes=ALIGN)
+            silu(activated[:], bank, m)
+            add_residual(m, c * CHUNK, CHUNK, activated[:])
+        nc.sync.dma_start(
+            out=out[0 : 2 * P, :].rearrange("(m p) s -> p m s", p=P),
+            in_=result_pair[:].rearrange("p (m s) -> p m s", m=2),
+        )
+
+        for m, slot, pieces in ((2, silu_slot_of[3], (S,)), (3, silu_slot_of[4], LAST_PIECES)):
+            activated_row = keep.tile([P, S], F32, name="activated_row", tag=slot, align_bytes=ALIGN)
+            for c in range(CHUNKS):
+                bank = second_product(m * CHUNKS + c, m, c)
+                silu(activated_row[:, c * CHUNK : (c + 1) * CHUNK], bank, m)
+                for piece, count in enumerate(pieces):
+                    first = sum(pieces[:piece])
+                    if c * CHUNK < first + count <= (c + 1) * CHUNK:
+                        cols = slice(first, first + count)
+                        add_residual(m, first, count, activated_row[:, cols])
+                        nc.sync.dma_start(out=out[P * m : P * (m + 1), cols], in_=result[m][:, cols])

@@ -1,7 +1,6 @@
 from contextlib import ExitStack
 
 import concourse.mybir as mybir
-from concourse.masks import make_identity
 
 K, M, T, S, H = 1024, 512, 4096, 1536, 512
 FLOPS = 2 * S * (K * H + H * M)
@@ -33,7 +32,7 @@ ALIGN = 256
 
 EARLY_PASS, LATE_PASS = 1, 0
 W1_LEAD = 3
-VECTOR_RELUS = (4, 6)
+VECTOR_RELUS = (5, 7)
 LAST_PIECES = (896, 448, 192)
 
 
@@ -56,9 +55,7 @@ def tile_list_tabres_silu_kernel(tc, tab_words, tab_scales, w1, w2_words, w2_sca
         resid = [keep.tile([P, T], F32, name=f"resid{m}", align_bytes=ALIGN) for m in range(ROW_TILES)]
         w2_codes = keep.tile([P, 2 * M], U8, name="w2_codes", align_bytes=ALIGN)
         w2_plane = v_plane[LATE_PASS][:, S : S + M]
-        bias_rows = keep.tile([P, P], F32, name="bias_rows", align_bytes=ALIGN)
-        identity = keep.tile([P, P], F32, name="identity")
-        bias = keep.tile([P, ROW_TILES], F32, name="bias")
+        bias_rows = keep.tile([P, QUADRANT], F32, name="bias_rows", align_bytes=ALIGN)
         w1_bf = [keep.tile([P, PACK * H], BF16, name=f"w1_bf{a}", align_bytes=ALIGN) for a in range(PASSES)]
         v_codes = [[None] * CHUNKS for a in range(PASSES)]
         w1_codes = [keep.tile([P, H], U32, name=f"w1_codes{a}", align_bytes=ALIGN) for a in range(PASSES)]
@@ -72,10 +69,9 @@ def tile_list_tabres_silu_kernel(tc, tab_words, tab_scales, w1, w2_words, w2_sca
 
         nc.vector.memset(tab_rows[:].bitcast(I32), 0)
         nc.vector.memset(w2_plane.bitcast(I32), 0)
-        nc.gpsimd.memset(bias_rows[:], 0.0)
+        nc.vector.memset(bias_rows[:], 0.0)
         warm = keep.tile([P, 1], F32, name="warm")
-        nc.scalar.activation(out=warm[:], in_=bias_rows[:, P - 1 : P], func=ACT.Silu)
-        make_identity(nc, identity[:])
+        nc.scalar.activation(out=warm[:], in_=bias_rows[:, 0:1], func=ACT.Silu)
 
         def w1_rows(a):
             return w1[PASS_ROWS * a : PASS_ROWS * (a + 1), :].rearrange("(p j) c -> p j c", j=PACK)
@@ -93,7 +89,10 @@ def tile_list_tabres_silu_kernel(tc, tab_words, tab_scales, w1, w2_words, w2_sca
 
         def gather_words(a, c):
             v_codes[a][c] = keep.tile([P, CHUNK], U32, name=f"v_codes{a}_{c}", align_bytes=ALIGN)
-            nc.vector.tensor_copy(out=v_codes[a][c][:], in_=tab[a][:].bitcast(U32).indirect(picks(c * CHUNK, CHUNK)))
+            count = CHUNK // 2 if (a, c) == (LATE_PASS, 0) else CHUNK
+            for first in range(0, CHUNK, count):
+                picked = tab[a][:].bitcast(U32).indirect(picks(c * CHUNK + first, count))
+                nc.vector.tensor_copy(out=v_codes[a][c][:, first : first + count], in_=picked)
 
         def round_w1(a):
             nc.scalar.copy(
@@ -102,7 +101,8 @@ def tile_list_tabres_silu_kernel(tc, tab_words, tab_scales, w1, w2_words, w2_sca
             )
 
         def quantise_w1(a):
-            w1_plane[a] = keep.tile([P, H], U8, name=f"w1_plane{a}", align_bytes=ALIGN)
+            tag = "v_rows" if a == EARLY_PASS else f"w1_plane{a}"
+            w1_plane[a] = keep.tile([P, H], U8, name=f"w1_plane{a}", tag=tag, align_bytes=ALIGN)
             nc.vector.quantize_mx(out=w1_codes[a][:].bitcast(FP8X4), scales=w1_plane[a][:], in_=w1_bf[a][:])
 
         nc.sync.dma_start(out=w1_raw[EARLY_PASS][:, 0:W1_LEAD, :], in_=w1_rows(EARLY_PASS)[:, 0:W1_LEAD, :])
@@ -112,7 +112,7 @@ def tile_list_tabres_silu_kernel(tc, tab_words, tab_scales, w1, w2_words, w2_sca
         nc.sync.dma_start(out=w1_raw[LATE_PASS][:], in_=w1_rows(LATE_PASS))
         load_tab(EARLY_PASS)
         nc.sync.dma_start(out=v_plane[LATE_PASS][0:P:8, S : S + M].bitcast(I32), in_=w2_scales[0].bitcast(I32))
-        nc.gpsimd.dma_start(out=bias_rows[0:ROW_TILES, :], in_=b.rearrange("(m p) -> m p", p=P))
+        nc.gpsimd.dma_start(out=bias_rows[0:P:8, :], in_=b.rearrange("(m q i) -> q m i", m=ROW_TILES, i=QUADRANT))
         nc.vector.tensor_copy(out=v_rows[:], in_=tab_rows[:].indirect(offsets[:]))
         place_scale_rows(EARLY_PASS)
         load_tab(LATE_PASS)
@@ -124,12 +124,11 @@ def tile_list_tabres_silu_kernel(tc, tab_words, tab_scales, w1, w2_words, w2_sca
         round_w1(EARLY_PASS)
         quantise_w1(EARLY_PASS)
         round_w1(LATE_PASS)
-        bias_bank = banks.tile([P, P], F32, name="bias_bank", tag=f"bank{BANKS - 1}")
-        nc.tensor.transpose(bias_bank[:], bias_rows[:], identity[:])
-        nc.scalar.copy(out=bias[:], in_=bias_bank[:, 0:ROW_TILES])
         quantise_w1(LATE_PASS)
         for c in range(CHUNKS):
             gather_words(EARLY_PASS, c)
+        bias = keep.tile([P, QUADRANT], F32, name="bias", tag=f"tab{EARLY_PASS}", align_bytes=ALIGN)
+        nc.vector.transpose(bias[:], bias_rows[:])
 
         h_bank_of = list(range(BANKS)) + [1, 5, 7, 0]
         y_rotation = (2, 7, 0, 5, 1)
@@ -175,7 +174,7 @@ def tile_list_tabres_silu_kernel(tc, tab_words, tab_scales, w1, w2_words, w2_sca
             return bank
 
         def silu(dest, bank, m):
-            nc.scalar.activation(out=dest, in_=bank[:], func=ACT.Silu, bias=bias[:, m : m + 1])
+            nc.scalar.activation(out=dest, in_=bank[:], func=ACT.Silu, bias=bias[:, 8 * m : 8 * m + 1])
 
         def add_residual(m, first, count, activated):
             picked = resid[m][:].indirect(picks(first, count))

@@ -31,9 +31,8 @@ BANKS = 8
 ALIGN = 256
 
 EARLY_PASS, LATE_PASS = 1, 0
-W1_LEAD = 3
 VECTOR_RELUS = (5, 7)
-LAST_PIECES = (896, 448, 192)
+LAST_PIECES = (1088, 448)
 
 
 def tile_list_tabres_silu_kernel(tc, tab_words, tab_scales, w1, w2_words, w2_scales, rT, b, offs, out):
@@ -105,14 +104,13 @@ def tile_list_tabres_silu_kernel(tc, tab_words, tab_scales, w1, w2_words, w2_sca
             w1_plane[a] = keep.tile([P, H], U8, name=f"w1_plane{a}", tag=tag, align_bytes=ALIGN)
             nc.vector.quantize_mx(out=w1_codes[a][:].bitcast(FP8X4), scales=w1_plane[a][:], in_=w1_bf[a][:])
 
-        nc.sync.dma_start(out=w1_raw[EARLY_PASS][:, 0:W1_LEAD, :], in_=w1_rows(EARLY_PASS)[:, 0:W1_LEAD, :])
+        nc.sync.dma_start(out=w1_raw[EARLY_PASS][:], in_=w1_rows(EARLY_PASS))
         nc.sync.dma_start(offsets[:], offs)
         nc.sync.dma_start(out=tab_rows[0:P:4, :].bitcast(I32), in_=tab_scales.rearrange("a q t -> q a t").bitcast(I32))
-        nc.sync.dma_start(out=w1_raw[EARLY_PASS][:, W1_LEAD:PACK, :], in_=w1_rows(EARLY_PASS)[:, W1_LEAD:PACK, :])
         nc.sync.dma_start(out=w1_raw[LATE_PASS][:], in_=w1_rows(LATE_PASS))
+        nc.sync.dma_start(out=bias_rows[0:P:8, :], in_=b.rearrange("(m q i) -> q m i", m=ROW_TILES, i=QUADRANT))
         load_tab(EARLY_PASS)
         nc.sync.dma_start(out=v_plane[LATE_PASS][0:P:8, S : S + M].bitcast(I32), in_=w2_scales[0].bitcast(I32))
-        nc.gpsimd.dma_start(out=bias_rows[0:P:8, :], in_=b.rearrange("(m q i) -> q m i", m=ROW_TILES, i=QUADRANT))
         nc.vector.tensor_copy(out=v_rows[:], in_=tab_rows[:].indirect(offsets[:]))
         place_scale_rows(EARLY_PASS)
         load_tab(LATE_PASS)

@@ -31,6 +31,7 @@ BANKS = 8
 ALIGN = 256
 
 EARLY_PASS, LATE_PASS = 1, 0
+W1_LEAD = 3
 VECTOR_RELUS = (5, 7)
 LAST_PIECES = (1088, 448)
 
@@ -104,9 +105,10 @@ def tile_list_tabres_silu_kernel(tc, tab_words, tab_scales, w1, w2_words, w2_sca
             w1_plane[a] = keep.tile([P, H], U8, name=f"w1_plane{a}", tag=tag, align_bytes=ALIGN)
             nc.vector.quantize_mx(out=w1_codes[a][:].bitcast(FP8X4), scales=w1_plane[a][:], in_=w1_bf[a][:])
 
-        nc.sync.dma_start(out=w1_raw[EARLY_PASS][:], in_=w1_rows(EARLY_PASS))
+        nc.sync.dma_start(out=w1_raw[EARLY_PASS][:, 0:W1_LEAD, :], in_=w1_rows(EARLY_PASS)[:, 0:W1_LEAD, :])
         nc.sync.dma_start(offsets[:], offs)
         nc.sync.dma_start(out=tab_rows[0:P:4, :].bitcast(I32), in_=tab_scales.rearrange("a q t -> q a t").bitcast(I32))
+        nc.sync.dma_start(out=w1_raw[EARLY_PASS][:, W1_LEAD:PACK, :], in_=w1_rows(EARLY_PASS)[:, W1_LEAD:PACK, :])
         nc.sync.dma_start(out=w1_raw[LATE_PASS][:], in_=w1_rows(LATE_PASS))
         nc.sync.dma_start(out=bias_rows[0:P:8, :], in_=b.rearrange("(m q i) -> q m i", m=ROW_TILES, i=QUADRANT))
         load_tab(EARLY_PASS)

@@ -31,7 +31,8 @@ BANKS = 8
 ALIGN = 256
 
 EARLY_PASS, LATE_PASS = 1, 0
-W1_LEAD = 3
+W1_LEAD = 1280
+SCALE_PARTS = ((0, 2 * CHUNK), (2 * CHUNK, S))
 VECTOR_RELUS = (5, 7)
 LAST_PIECES = (1088, 448)
 
@@ -51,7 +52,7 @@ def tile_list_tabres_silu_kernel(tc, tab_words, tab_scales, w1, w2_words, w2_sca
         v_rows = keep.tile([P, S], U8, name="v_rows", align_bytes=ALIGN)
         v_plane = [keep.tile([P, S + (M if a == LATE_PASS else 0)], U8, name=f"v_plane{a}", align_bytes=ALIGN) for a in range(PASSES)]
         tab = [keep.tile([P, T], I32, name=f"tab{a}", align_bytes=ALIGN) for a in range(PASSES)]
-        w1_raw = [keep.tile([P, PACK, H], F32, name=f"w1_raw{a}", align_bytes=ALIGN) for a in range(PASSES)]
+        w1_raw = [keep.tile([P, PACK * H], F32, name=f"w1_raw{a}", align_bytes=ALIGN) for a in range(PASSES)]
         resid = [keep.tile([P, T], F32, name=f"resid{m}", align_bytes=ALIGN) for m in range(ROW_TILES)]
         w2_codes = keep.tile([P, 2 * M], U8, name="w2_codes", align_bytes=ALIGN)
         w2_plane = v_plane[LATE_PASS][:, S : S + M]
@@ -73,14 +74,16 @@ def tile_list_tabres_silu_kernel(tc, tab_words, tab_scales, w1, w2_words, w2_sca
         warm = keep.tile([P, 1], F32, name="warm")
         nc.scalar.activation(out=warm[:], in_=bias_rows[:, 0:1], func=ACT.Silu)
 
-        def w1_rows(a):
-            return w1[PASS_ROWS * a : PASS_ROWS * (a + 1), :].rearrange("(p j) c -> p j c", j=PACK)
+        def load_w1(a, first, last):
+            rows = w1[PASS_ROWS * a : PASS_ROWS * (a + 1), :].rearrange("(p j) c -> p (j c)", j=PACK)
+            nc.sync.dma_start(out=w1_raw[a][:, first:last], in_=rows[:, first:last])
 
         def load_tab(a):
             nc.sync.dma_start(out=tab[a][:], in_=tab_words[a].rearrange("p t i -> p (t i)").bitcast(I32))
 
         def place_scale_rows(a):
-            nc.vector.tensor_copy(out=v_plane[a][:, 0:S].bitcast(I32), in_=v_rows[:].bitcast(I32))
+            for first, last in SCALE_PARTS if a == EARLY_PASS else ((0, S),):
+                nc.vector.tensor_copy(out=v_plane[a][:, first:last].bitcast(I32), in_=v_rows[:, first:last].bitcast(I32))
             for row in range(1, 4):
                 nc.sync.dma_start(
                     out=v_plane[a][4 * a + row : P : QUADRANT, :].bitcast(I32),
@@ -97,7 +100,7 @@ def tile_list_tabres_silu_kernel(tc, tab_words, tab_scales, w1, w2_words, w2_sca
         def round_w1(a):
             nc.scalar.copy(
                 out=w1_bf[a][:].rearrange("p (t i j) -> p i t j", t=PACK, j=PACK),
-                in_=w1_raw[a][:].rearrange("p j (i t) -> p i t j", t=PACK),
+                in_=w1_raw[a][:].rearrange("p (j i t) -> p i t j", j=PACK, t=PACK),
             )
 
         def quantise_w1(a):
@@ -105,15 +108,16 @@ def tile_list_tabres_silu_kernel(tc, tab_words, tab_scales, w1, w2_words, w2_sca
             w1_plane[a] = keep.tile([P, H], U8, name=f"w1_plane{a}", tag=tag, align_bytes=ALIGN)
             nc.vector.quantize_mx(out=w1_codes[a][:].bitcast(FP8X4), scales=w1_plane[a][:], in_=w1_bf[a][:])
 
-        nc.sync.dma_start(out=w1_raw[EARLY_PASS][:, 0:W1_LEAD, :], in_=w1_rows(EARLY_PASS)[:, 0:W1_LEAD, :])
+        load_w1(EARLY_PASS, 0, W1_LEAD)
         nc.sync.dma_start(offsets[:], offs)
         nc.sync.dma_start(out=tab_rows[0:P:4, :].bitcast(I32), in_=tab_scales.rearrange("a q t -> q a t").bitcast(I32))
-        nc.sync.dma_start(out=w1_raw[EARLY_PASS][:, W1_LEAD:PACK, :], in_=w1_rows(EARLY_PASS)[:, W1_LEAD:PACK, :])
-        nc.sync.dma_start(out=w1_raw[LATE_PASS][:], in_=w1_rows(LATE_PASS))
+        load_w1(EARLY_PASS, W1_LEAD, PACK * H)
+        load_w1(LATE_PASS, 0, PACK * H)
         nc.sync.dma_start(out=bias_rows[0:P:8, :], in_=b.rearrange("(m q i) -> q m i", m=ROW_TILES, i=QUADRANT))
         load_tab(EARLY_PASS)
         nc.sync.dma_start(out=v_plane[LATE_PASS][0:P:8, S : S + M].bitcast(I32), in_=w2_scales[0].bitcast(I32))
-        nc.vector.tensor_copy(out=v_rows[:], in_=tab_rows[:].indirect(offsets[:]))
+        for first, last in SCALE_PARTS:
+            nc.vector.tensor_copy(out=v_rows[:, first:last], in_=tab_rows[:].indirect(picks(first, last - first)))
         place_scale_rows(EARLY_PASS)
         load_tab(LATE_PASS)
         place_scale_rows(LATE_PASS)

@@ -33,7 +33,7 @@ ALIGN = 256
 EARLY_PASS, LATE_PASS = 1, 0
 W1_LEAD = 1280
 SCALE_PARTS = ((0, 2 * CHUNK), (2 * CHUNK, S))
-VECTOR_RELUS = (5, 7)
+VECTOR_RELUS = (5, 7, 9)
 LAST_PIECES = (1088, 448)
 
 

@@ -32,7 +32,6 @@ ALIGN = 256
 
 EARLY_PASS, LATE_PASS = 1, 0
 W1_LEAD = 1280
-SCALE_PARTS = ((0, 2 * CHUNK), (2 * CHUNK, S))
 VECTOR_RELUS = (5, 7, 9)
 LAST_PIECES = (1088, 448)
 
@@ -82,8 +81,7 @@ def tile_list_tabres_silu_kernel(tc, tab_words, tab_scales, w1, w2_words, w2_sca
             nc.sync.dma_start(out=tab[a][:], in_=tab_words[a].rearrange("p t i -> p (t i)").bitcast(I32))
 
         def place_scale_rows(a):
-            for first, last in SCALE_PARTS if a == EARLY_PASS else ((0, S),):
-                nc.vector.tensor_copy(out=v_plane[a][:, first:last].bitcast(I32), in_=v_rows[:, first:last].bitcast(I32))
+            nc.vector.tensor_copy(out=v_plane[a][:, 0:S].bitcast(I32), in_=v_rows[:].bitcast(I32))
             for row in range(1, 4):
                 nc.sync.dma_start(
                     out=v_plane[a][4 * a + row : P : QUADRANT, :].bitcast(I32),
@@ -116,8 +114,7 @@ def tile_list_tabres_silu_kernel(tc, tab_words, tab_scales, w1, w2_words, w2_sca
         nc.sync.dma_start(out=bias_rows[0:P:8, :], in_=b.rearrange("(m q i) -> q m i", m=ROW_TILES, i=QUADRANT))
         load_tab(EARLY_PASS)
         nc.sync.dma_start(out=v_plane[LATE_PASS][0:P:8, S : S + M].bitcast(I32), in_=w2_scales[0].bitcast(I32))
-        for first, last in SCALE_PARTS:
-            nc.vector.tensor_copy(out=v_rows[:, first:last], in_=tab_rows[:].indirect(picks(first, last - first)))
+        nc.vector.tensor_copy(out=v_rows[:], in_=tab_rows[:].indirect(offsets[:]))
         place_scale_rows(EARLY_PASS)
         load_tab(LATE_PASS)
         place_scale_rows(LATE_PASS)

from contextlib import ExitStack

import concourse.mybir as mybir

K, M, T, S, H = 1024, 512, 4096, 1536, 512
FLOPS = 2 * S * (K * H + H * M)

F32 = mybir.dt.float32
BF16 = mybir.dt.bfloat16
I32 = mybir.dt.int32
U32 = mybir.dt.uint32
U16 = mybir.dt.uint16
U8 = mybir.dt.uint8
FP8X4 = mybir.dt.float8_e4m3fn_x4
FP4X4 = mybir.dt.float4_e2m1fn_x4
ACT = mybir.ActivationFunctionType
ADD = mybir.AluOpType.add

P = 128
PACK = 4
PASS_ROWS = P * PACK
PASSES = K // PASS_ROWS
CHUNK = 512
CHUNKS = S // CHUNK
GROUP = CHUNK // PACK
GROUPS_PER_CHUNK = CHUNK // GROUP
ROW_TILES = M // P
PER_COLUMN = 16
QUADRANT = 32
BANKS = 8
ALIGN = 256

EARLY_PASS, LATE_PASS = 1, 0
W1_LEAD = 1280
VECTOR_RELUS = (5, 7, 9)
LAST_PIECES = (1088, 448)


def tile_list_tabres_silu_kernel(tc, tab_words, tab_scales, w1, w2_words, w2_scales, rT, b, offs, out):
    nc = tc.nc
    with ExitStack() as ctx:
        keep = ctx.enter_context(tc.tile_pool(name="keep", bufs=1))
        banks = ctx.enter_context(tc.psum_pool(name="banks", bufs=1))

        offsets = keep.tile([P, S // PER_COLUMN], U16, name="offsets", align_bytes=ALIGN)

        def picks(first, count):
            return offsets[:, first // PER_COLUMN : (first + count) // PER_COLUMN]

        tab_rows = keep.tile([P, T], U8, name="tab_rows", align_bytes=ALIGN)
        v_rows = keep.tile([P, S], U8, name="v_rows", align_bytes=ALIGN)
        v_plane = [keep.tile([P, S + (M if a == LATE_PASS else 0)], U8, name=f"v_plane{a}", align_bytes=ALIGN) for a in range(PASSES)]
        tab = [keep.tile([P, T], I32, name=f"tab{a}", align_bytes=ALIGN) for a in range(PASSES)]
        w1_raw = [keep.tile([P, PACK * H], F32, name=f"w1_raw{a}", align_bytes=ALIGN) for a in range(PASSES)]
        resid = [keep.tile([P, T], F32, name=f"resid{m}", align_bytes=ALIGN) for m in range(ROW_TILES)]
        w2_codes = keep.tile([P, 2 * M], U8, name="w2_codes", align_bytes=ALIGN)
        w2_plane = v_plane[LATE_PASS][:, S : S + M]
        bias_rows = keep.tile([P, QUADRANT], F32, name="bias_rows", align_bytes=ALIGN)
        w1_bf = [keep.tile([P, PACK * H], BF16, name=f"w1_bf{a}", align_bytes=ALIGN) for a in range(PASSES)]
        v_codes = [[None] * CHUNKS for a in range(PASSES)]
        w1_codes = [keep.tile([P, H], U32, name=f"w1_codes{a}", align_bytes=ALIGN) for a in range(PASSES)]
        w1_plane = [None] * PASSES
        h_bf = [keep.tile([P, PACK * CHUNK], BF16, name=f"h_bf{c}", align_bytes=ALIGN) for c in range(CHUNKS)]
        h_codes = [None] * CHUNKS
        h_plane = [keep.tile([P, CHUNK], U8, name=f"h_plane{c}", align_bytes=ALIGN) for c in range(CHUNKS)]
        result_pair = keep.tile([P, 2 * S], F32, name="result_pair", align_bytes=ALIGN)
        result = [result_pair[:, 0:S], result_pair[:, S : 2 * S]]
        result += [keep.tile([P, S], F32, name=f"result{m}", align_bytes=ALIGN)[:] for m in range(2, ROW_TILES)]

        nc.vector.memset(tab_rows[:].bitcast(I32), 0)
        nc.vector.memset(w2_plane.bitcast(I32), 0)
        nc.vector.memset(bias_rows[:], 0.0)
        warm = keep.tile([P, 1], F32, name="warm")
        nc.scalar.activation(out=warm[:], in_=bias_rows[:, 0:1], func=ACT.Silu)

        def load_w1(a, first, last):
            rows = w1[PASS_ROWS * a : PASS_ROWS * (a + 1), :].rearrange("(p j) c -> p (j c)", j=PACK)
            nc.sync.dma_start(out=w1_raw[a][:, first:last], in_=rows[:, first:last])

        def load_tab(a):
            nc.sync.dma_start(out=tab[a][:], in_=tab_words[a].rearrange("p t i -> p (t i)").bitcast(I32))

        def place_scale_rows(a):
            nc.vector.tensor_copy(out=v_plane[a][:, 0:S].bitcast(I32), in_=v_rows[:].bitcast(I32))
            for row in range(1, 4):
                nc.sync.dma_start(
                    out=v_plane[a][4 * a + row : P : QUADRANT, :].bitcast(I32),
                    in_=v_plane[a][4 * a + 8 * row : P : QUADRANT, :].bitcast(I32),
                )

        def gather_words(a, c):
            v_codes[a][c] = keep.tile([P, CHUNK], U32, name=f"v_codes{a}_{c}", align_bytes=ALIGN)
            count = CHUNK // 2 if (a, c) == (LATE_PASS, 0) else CHUNK
            for first in range(0, CHUNK, count):
                picked = tab[a][:].bitcast(U32).indirect(picks(c * CHUNK + first, count))
                nc.vector.tensor_copy(out=v_codes[a][c][:, first : first + count], in_=picked)

        def round_w1(a):
            nc.scalar.copy(
                out=w1_bf[a][:].rearrange("p (t i j) -> p i t j", t=PACK, j=PACK),
                in_=w1_raw[a][:].rearrange("p (j i t) -> p i t j", j=PACK, t=PACK),
            )

        def quantise_w1(a):
            tag = "v_rows" if a == EARLY_PASS else f"w1_plane{a}"
            w1_plane[a] = keep.tile([P, H], U8, name=f"w1_plane{a}", tag=tag, align_bytes=ALIGN)
            nc.vector.quantize_mx(out=w1_codes[a][:].bitcast(FP8X4), scales=w1_plane[a][:], in_=w1_bf[a][:])

        load_w1(EARLY_PASS, 0, W1_LEAD)
        nc.sync.dma_start(offsets[:], offs)
        nc.sync.dma_start(out=tab_rows[0:P:4, :].bitcast(I32), in_=tab_scales.rearrange("a q t -> q a t").bitcast(I32))
        load_w1(EARLY_PASS, W1_LEAD, PACK * H)
        load_w1(LATE_PASS, 0, PACK * H)
        nc.sync.dma_start(out=bias_rows[0:P:8, :], in_=b.rearrange("(m q i) -> q m i", m=ROW_TILES, i=QUADRANT))
        load_tab(EARLY_PASS)
        nc.sync.dma_start(out=v_plane[LATE_PASS][0:P:8, S : S + M].bitcast(I32), in_=w2_scales[0].bitcast(I32))
        nc.vector.tensor_copy(out=v_rows[:], in_=tab_rows[:].indirect(offsets[:]))
        place_scale_rows(EARLY_PASS)
        load_tab(LATE_PASS)
        place_scale_rows(LATE_PASS)
        nc.sync.dma_start(out=w2_codes[:].bitcast(I32), in_=w2_words[0].bitcast(I32))
        for m in range(ROW_TILES):
            nc.sync.dma_start(out=resid[m][:], in_=rT[P * m : P * (m + 1), :])

        round_w1(EARLY_PASS)
        quantise_w1(EARLY_PASS)
        round_w1(LATE_PASS)
        quantise_w1(LATE_PASS)
        for c in range(CHUNKS):
            gather_words(EARLY_PASS, c)
        bias = keep.tile([P, QUADRANT], F32, name="bias", tag=f"tab{EARLY_PASS}", align_bytes=ALIGN)
        nc.vector.transpose(bias[:], bias_rows[:])

        h_bank_of = list(range(BANKS)) + [1, 5, 7, 0]
        y_rotation = (2, 7, 0, 5, 1)
        silu_slot_of = ("slot_first", "slot_b", "slot_a", "slot_b", "slot_a", "slot_sixth")

        def first_layer(group):
            c, g = divmod(group, GROUPS_PER_CHUNK)
            cols = slice(g * GROUP, (g + 1) * GROUP)
            bank = banks.tile([P, PACK, GROUP], F32, name="h_bank", tag=f"bank{h_bank_of[group]}")
            for a in (EARLY_PASS, LATE_PASS):
                for t in range(PACK):
                    nc.tensor.matmul_mx(
                        out=bank[:, t, :],
                        lhsT=w1_codes[a][:, P * t : P * (t + 1)].bitcast(FP8X4),
                        lhsT_scale=w1_plane[a][:, P * t : P * (t + 1)],
                        rhs=v_codes[a][c][:, cols].bitcast(FP8X4),
                        rhs_scale=v_plane[a][4 * a : P, group * GROUP : (group + 1) * GROUP],
                        start=(a == EARLY_PASS and t == 0),
                        stop=(a == LATE_PASS and t == PACK - 1),
                    )
            woven = h_bf[c][:, PACK * GROUP * g : PACK * GROUP * (g + 1)].rearrange("p (n t) -> p n t", t=PACK)
            sums = bank[:].rearrange("p t n -> p n t")
            if group in VECTOR_RELUS:
                nc.vector.tensor_scalar_max(woven, sums, 0.0)
            else:
                nc.scalar.activation(out=woven, in_=sums, func=ACT.Relu)
            if g == GROUPS_PER_CHUNK - 1:
                tag = silu_slot_of[0] if c == CHUNKS - 1 else f"h_codes{c}"
                h_codes[c] = keep.tile([P, CHUNK], U32, name=f"h_codes{c}", tag=tag, align_bytes=ALIGN)
                nc.vector.quantize_mx(out=h_codes[c][:].bitcast(FP8X4), scales=h_plane[c][:], in_=h_bf[c][:])

        def second_product(step, m, c):
            bank = banks.tile([P, CHUNK], F32, name="y_bank", tag=f"bank{y_rotation[(step - 1) % len(y_rotation)] if step else 0}")
            nc.tensor.matmul_mx(
                out=bank[:],
                lhsT=w2_codes[:, 2 * P * m : 2 * P * (m + 1)].bitcast(FP4X4),
                lhsT_scale=v_plane[LATE_PASS][:, S + P * m : S + P * (m + 1)],
                rhs=h_codes[c][:].bitcast(FP8X4),
                rhs_scale=h_plane[c][:],
                start=True,
                stop=True,
            )
            return bank

        def silu(dest, bank, m):
            nc.scalar.activation(out=dest, in_=bank[:], func=ACT.Silu, bias=bias[:, 8 * m : 8 * m + 1])

        def add_residual(m, first, count, activated):
            picked = resid[m][:].indirect(picks(first, count))
            nc.vector.tensor_tensor(out=result[m][:, first : first + count], in0=picked, in1=activated, op=ADD)

        for c in range(CHUNKS):
            gather_words(LATE_PASS, c)

        pair_steps = [(m, c) for m in range(2) for c in range(CHUNKS - 1)] + [(m, CHUNKS - 1) for m in range(2)]
        groups_before = {0: range(0, 8), 1: range(8, 10), 2: range(10, 12)}
        for step, (m, c) in enumerate(pair_steps):
            for group in groups_before.get(step, ()):
                first_layer(group)
            bank = second_product(step, m, c)
            activated = keep.tile([P, CHUNK], F32, name="activated", tag=silu_slot_of[step], align_bytes=ALIGN)
            silu(activated[:], bank, m)
            add_residual(m, c * CHUNK, CHUNK, activated[:])
        nc.sync.dma_start(
            out=out[0 : 2 * P, :].rearrange("(m p) s -> p m s", p=P),
            in_=result_pair[:].rearrange("p (m s) -> p m s", m=2),
        )

        for m, slot, pieces in ((2, silu_slot_of[3], (S,)), (3, silu_slot_of[4], LAST_PIECES)):
            activated_row = keep.tile([P, S], F32, name="activated_row", tag=slot, align_bytes=ALIGN)
            for c in range(CHUNKS):
                bank = second_product(m * CHUNKS + c, m, c)
                silu(activated_row[:, c * CHUNK : (c + 1) * CHUNK], bank, m)
                for piece, count in enumerate(pieces):
                    first = sum(pieces[:piece])
                    if c * CHUNK < first + count <= (c + 1) * CHUNK:
                        cols = slice(first, first + count)
                        add_residual(m, first, count, activated_row[:, cols])
                        nc.sync.dma_start(out=out[P * m : P * (m + 1), cols], in_=result[m][:, cols])
